import numpy as np
import ml_dtypes


def mxq(x, axis, fmt="e4m3"):
    dtype, down = {"e4m3": (ml_dtypes.float8_e4m3fn, 7), "e5m2": (ml_dtypes.float8_e5m2, 14)}[fmt]
    v = np.moveaxis(np.asarray(x, np.float32).astype(ml_dtypes.bfloat16).astype(np.float64), axis, -1)
    blocks = v.reshape(v.shape[:-1] + (-1, 32))
    amax = np.abs(blocks).max(-1, keepdims=True)
    byte = np.maximum(np.where(amax > 0, np.frexp(amax)[1] - 1 + 127, 0) - down, 1)
    scale = np.exp2(byte - 127.0)
    codes = (blocks / scale).astype(np.float32).astype(dtype).astype(np.float64)
    return np.moveaxis((codes * scale).reshape(v.shape), -1, axis)


WIDE = False


def mx_kscale(k):
    if not WIDE:
        return np.ones(k)
    levels = np.array([18, -18])
    if k % 512:
        return np.exp2(np.random.permutation(np.resize(levels, k // 32))).repeat(32)
    a = np.empty((k // 512, 16))
    for p in range(k // 512):
        a[p, :8] = np.random.permutation(np.resize(levels, 8))
        for g in range(8):
            far = levels[np.abs(levels - a[p, g]) >= 10]
            a[p, g + 8] = far[np.random.randint(len(far))]
    return np.exp2(a.ravel()).repeat(32)


def f64(x):
    return np.asarray(x).astype(np.float64)


def striped(idx):
    return np.tile(np.asarray(idx).reshape(-1, 16).T, (8, 1)).astype(np.uint16)


def unstriped(offs):
    return offs[:16].T.reshape(-1).astype(np.int64)


B, N, T, D, R = 1, 512, 2048, 512, 512
PAGE = 64


def setup_inputs():
    n = np.random.standard_normal
    pages = np.random.permutation(T // PAGE)[:B * N // PAGE]
    idx = (pages[:, None] * PAGE + np.arange(PAGE)[None, :]).reshape(-1)
    s = mx_kscale(D)[:, None]
    z = mx_kscale(R)[:, None]
    q = n((B, D, R))
    do = n((B, D, R))
    return {
        "qT": (q * s).astype(np.float32),
        "cT": (n((D, T)) * (1.00 / np.sqrt(D)) / s).astype(np.float32),
        "doT": (do * s).astype(np.float32),
        "rw": (np.random.uniform(0.5, 1.5, (B, R, 1)) * 1.0 / np.sqrt(R) * z).astype(np.float32),
        "qm": (q.transpose(0, 2, 1) / z).astype(np.float32),
        "dom": (do.transpose(0, 2, 1) / z).astype(np.float32),
        "offs": striped(idx),
    }


def reference(qT, cT, doT, rw, qm, dom, offs):
    idx = unstriped(offs)
    pick = lambda x: x[:, idx].reshape(x.shape[0], B, N).transpose(1, 0, 2)
    cq = mxq(pick(f64(cT)), 1, "e4m3")
    a = mxq(f64(qT), 1, "e4m3").transpose(0, 2, 1) @ cq
    p = np.tanh(a)
    dp = mxq(f64(doT), 1, "e5m2").transpose(0, 2, 1) @ cq
    ds = f64(rw) * dp * (1.0 - p * p)
    dk = mxq(f64(qm), 1, "e4m3").transpose(0, 2, 1) @ mxq(ds, 1, "e5m2")
    dv = mxq(f64(dom), 1, "e5m2").transpose(0, 2, 1) @ mxq(f64(rw) * p, 1, "e4m3")
    gc = np.zeros((D, T))
    gc[:, idx] = (dk + dv).transpose(1, 0, 2).reshape(D, B * N)
    return gc

@@ -1,0 +1,151 @@
+from contextlib import ExitStack
+
+import concourse.mybir as mybir
+
+N, T, D, R = 512, 2048, 512, 512
+FLOPS = 4 * 2 * D * R * N
+
+F32 = mybir.dt.float32
+BF16 = mybir.dt.bfloat16
+U32 = mybir.dt.uint32
+U16 = mybir.dt.uint16
+U8 = mybir.dt.uint8
+E4M3 = mybir.dt.float8_e4m3fn_x4
+E5M2 = mybir.dt.float8_e5m2_x4
+ACT = mybir.ActivationFunctionType
+ALU = mybir.AluOpType
+
+P = 128
+PACK = 4
+Q_SPLIT = 88
+
+
+def tile_attend_gat_tnh_c_kernel(tc, qT, cT, doT, rw, qm, dom, offs, out):
+    nc = tc.nc
+    with ExitStack() as ctx:
+        keep = ctx.enter_context(tc.tile_pool(name="keep", bufs=1))
+        psum = ctx.enter_context(tc.psum_pool(name="psum", bufs=1))
+
+        def sbuf(name, shape, dtype):
+            return keep.tile(shape, dtype, name=name, align_bytes=64)
+
+        def operand(name, width):
+            return sbuf(name + "_codes", [P, width], U32), sbuf(name + "_scales", [P, width], U8)
+
+        def quantize(dst, src, fmt, lo, hi):
+            codes, scales = dst
+            nc.vector.quantize_mx(out=codes[:, lo:hi].bitcast(fmt), scales=scales[:, lo:hi],
+                                  in_=src[:, PACK * lo : PACK * hi])
+
+        def product(bank, stationary, stationary_fmt, lo, moving, moving_fmt, start, stop):
+            nc.tensor.matmul_mx(out=bank[:], lhsT=stationary[0][:, lo : lo + P].bitcast(stationary_fmt),
+                                lhsT_scale=stationary[1][:, lo : lo + P],
+                                rhs=moving[0][:].bitcast(moving_fmt), rhs_scale=moving[1][:],
+                                start=start, stop=stop)
+
+        def weave(copy, dst, src, lo, hi):
+            copy(out=dst[:, PACK * lo : PACK * hi].rearrange("p (c i t) -> p c t i", i=4, t=PACK),
+                 in_=src[:, :, lo:hi].rearrange("p t (c i) -> p c t i", i=4))
+
+        def deal(copy, dst, src, lo, hi):
+            copy(out=dst[:].rearrange("p (t s j) -> p s j t", t=PACK, j=PACK)[:, lo:hi],
+                 in_=src[:].rearrange("p j (s t) -> p s j t", t=PACK)[:, lo:hi])
+
+        offsets = sbuf("offsets", [P, N // 16], U16)
+        nc.sync.dma_start(offsets[:], offs)
+        planes = [sbuf("plane%d" % t, [P, T], F32) for t in range(PACK)]
+        c_rows = cT.rearrange("(p t) n -> t p n", t=PACK)
+        for t in range(PACK):
+            nc.sync.dma_start(out=planes[t][:], in_=c_rows[t])
+        gate = sbuf("gate", [P, PACK], F32)
+        nc.sync.dma_start(out=gate[:], in_=rw[0].rearrange("(p t) o -> p (t o)", t=PACK))
+        raw = {}
+        for name, src in (("qT", qT), ("doT", doT), ("qm", qm), ("dom", dom)):
+            raw[name] = sbuf(name + "_raw", [P, PACK, 512], F32)
+            nc.sync.dma_start(out=raw[name][:], in_=src[0].rearrange("(p j) w -> p j w", j=PACK))
+
+        windows = [sbuf("window%d" % j, [P, T], F32) for j in range(D // P)]
+        for j in range(D // P):
+            nc.vector.memset(windows[j][:], 0.0)
+        warm_in = sbuf("warm_in", [P, 8], F32)
+        warm_out = sbuf("warm_out", [P, 8], F32)
+        nc.gpsimd.memset(warm_in[:], 0.0)
+        nc.scalar.activation(out=warm_out[:], in_=warm_in[:], func=ACT.Tanh)
+
+        c_woven = sbuf("c_woven", [P, N * PACK], BF16)
+        c_places = c_woven[:].rearrange("p (n t) -> p t n", t=PACK)
+        for t in range(PACK):
+            nc.vector.tensor_copy(c_places[:, t, :], planes[t][:].indirect(offsets[:]))
+        c_mx = operand("c", N)
+        quantize(c_mx, c_woven, E4M3, 0, N)
+        neg_gate = sbuf("neg_gate", [P, PACK], F32)
+        nc.vector.tensor_scalar(neg_gate[:], gate[:], -1.0, None, ALU.mult)
+
+        qT_woven = sbuf("qT_woven", [P, R * PACK], BF16)
+        deal(nc.scalar.copy, qT_woven, raw["qT"], Q_SPLIT, P)
+        deal(nc.vector.tensor_copy, qT_woven, raw["qT"], 0, Q_SPLIT)
+        qT_mx = operand("qT", R)
+        scores = []
+        for t in range(PACK):
+            quantize(qT_mx, qT_woven, E4M3, t * P, (t + 1) * P)
+            bank = psum.tile([P, N], F32, name="first%d" % t)
+            product(bank, qT_mx, E4M3, t * P, c_mx, E4M3, True, True)
+            scores.append(bank)
+
+        doT_woven = sbuf("doT_woven", [P, R * PACK], BF16)
+        deal(nc.vector.tensor_copy, doT_woven, raw["doT"], 0, P)
+        doT_mx = operand("doT", R)
+        dp = []
+        for t in range(PACK):
+            quantize(doT_mx, doT_woven, E5M2, t * P, (t + 1) * P)
+            bank = psum.tile([P, N], F32, name="second%d" % t)
+            product(bank, doT_mx, E5M2, t * P, c_mx, E4M3, True, True)
+            dp.append(bank)
+
+        ds = sbuf("ds", [P, PACK, N], BF16)
+        pw = sbuf("pw", [P, PACK, N], BF16)
+        p = [sbuf("p%d" % t, [P, N], F32) for t in range(PACK)]
+        for t in range(PACK):
+            p_sq = sbuf("p_sq%d" % t, [P, N], F32)
+            slope = sbuf("slope%d" % t, [P, N], F32)
+            nc.scalar.activation(out=p[t][:], in_=scores[t][:], func=ACT.Tanh)
+            nc.scalar.activation(out=p_sq[:], in_=p[t][:], func=ACT.Square)
+            nc.vector.tensor_scalar(slope[:], p_sq[:], neg_gate[:, t : t + 1], gate[:, t : t + 1], ALU.mult, ALU.add)
+            if t < 3:
+                nc.vector.tensor_scalar(pw[:, t, :], p[t][:], gate[:, t : t + 1], None, ALU.mult)
+            else:
+                nc.scalar.activation(out=pw[:, t, :], in_=p[t][:], func=ACT.Copy, scale=gate[:, t : t + 1])
+            nc.vector.tensor_tensor(ds[:, t, :], dp[t][:], slope[:], ALU.mult)
+
+        pw_woven = sbuf("pw_woven", [P, N * PACK], BF16)
+        ds_woven = sbuf("ds_woven", [P, N * PACK], BF16)
+        qm_woven = sbuf("qm_woven", [P, D * PACK], BF16)
+        dom_woven = sbuf("dom_woven", [P, D * PACK], BF16)
+        pw_mx = operand("pw", N)
+        ds_mx = operand("ds", N)
+        qm_mx = operand("qm", D)
+        dom_mx = operand("dom", D)
+
+        weave(nc.scalar.copy, pw_woven, pw, 0, N)
+        weave(nc.vector.tensor_copy, ds_woven, ds, 0, N)
+        weave(nc.vector.tensor_copy, qm_woven, raw["qm"], 0, P)
+        weave(nc.vector.tensor_copy, dom_woven, raw["dom"], 0, P)
+        quantize(ds_mx, ds_woven, E5M2, 0, N)
+        quantize(qm_mx, qm_woven, E4M3, 0, P)
+        quantize(dom_mx, dom_woven, E5M2, 0, P)
+        quantize(pw_mx, pw_woven, E4M3, 0, N)
+
+        for j in range(D // P):
+            lo, hi = j * P, (j + 1) * P
+            bank = psum.tile([P, N], F32, name="first%d" % j)
+            product(bank, qm_mx, E4M3, lo, ds_mx, E5M2, True, False)
+            product(bank, dom_mx, E5M2, lo, pw_mx, E4M3, False, True)
+            if hi < D:
+                weave(nc.scalar.copy, qm_woven, raw["qm"], hi, hi + P)
+                weave(nc.scalar.copy, dom_woven, raw["dom"], hi, hi + P)
+                quantize(qm_mx, qm_woven, E4M3, hi, hi + P)
+                quantize(dom_mx, dom_woven, E5M2, hi, hi + P)
+            result = sbuf("result%d" % j, [P, N], F32)
+            nc.scalar.copy(out=result[:], in_=bank[:])
+            nc.vector.tensor_copy(windows[j][:].indirect(offsets[:]), result[:])
+            nc.sync.dma_start(out=out[lo:hi, :], in_=windows[j][:])

@@ -17,7 +17,12 @@ ALU = mybir.AluOpType
 
 P = 128
 PACK = 4
-Q_SPLIT = 88
+BAND = 16
+RUN = 4
+Q_SPLIT = 80
+PW_SPLIT = 256
+DS_SPLIT = 256
+EVH = 0
 
 
 def tile_attend_gat_tnh_c_kernel(tc, qT, cT, doT, rw, qm, dom, offs, out):
@@ -43,45 +48,48 @@ def tile_attend_gat_tnh_c_kernel(tc, qT, cT, doT, rw, qm, dom, offs, out):
                                 rhs=moving[0][:].bitcast(moving_fmt), rhs_scale=moving[1][:],
                                 start=start, stop=stop)
 
-        def weave(copy, dst, src, lo, hi):
-            copy(out=dst[:, PACK * lo : PACK * hi].rearrange("p (c i t) -> p c t i", i=4, t=PACK),
-                 in_=src[:, :, lo:hi].rearrange("p t (c i) -> p c t i", i=4))
+        def weave(copy, dst, src):
+            copy(out=dst.rearrange("p (c i t) -> p c t i", i=RUN, t=PACK),
+                 in_=src.rearrange("p t (c i) -> p c t i", i=RUN))
 
         def deal(copy, dst, src, lo, hi):
             copy(out=dst[:].rearrange("p (t s j) -> p s j t", t=PACK, j=PACK)[:, lo:hi],
                  in_=src[:].rearrange("p j (s t) -> p s j t", t=PACK)[:, lo:hi])
 
-        offsets = sbuf("offsets", [P, N // 16], U16)
-        nc.sync.dma_start(offsets[:], offs)
+        halves = [(0, N // 2), (N // 2, N)]
+
+        offsets = sbuf("offsets", [P, N // BAND], U16)
         planes = [sbuf("plane%d" % t, [P, T], F32) for t in range(PACK)]
         c_rows = cT.rearrange("(p t) n -> t p n", t=PACK)
-        for t in range(PACK):
+        nc.sync.dma_start(out=planes[0][:], in_=c_rows[0])
+        nc.sync.dma_start(offsets[:], offs)
+        for t in range(1, PACK):
             nc.sync.dma_start(out=planes[t][:], in_=c_rows[t])
         gate = sbuf("gate", [P, PACK], F32)
-        nc.sync.dma_start(out=gate[:], in_=rw[0].rearrange("(p t) o -> p (t o)", t=PACK))
+        nc.scalar.dma_start(out=gate[:], in_=rw[0].rearrange("(p t) o -> p (t o)", t=PACK))
         raw = {}
-        for name, src in (("qT", qT), ("doT", doT), ("qm", qm), ("dom", dom)):
+        for name, src in (("qT", qT), ("doT", doT), ("dom", dom), ("qm", qm)):
             raw[name] = sbuf(name + "_raw", [P, PACK, 512], F32)
             nc.sync.dma_start(out=raw[name][:], in_=src[0].rearrange("(p j) w -> p j w", j=PACK))
 
         windows = [sbuf("window%d" % j, [P, T], F32) for j in range(D // P)]
         for j in range(D // P):
-            nc.vector.memset(windows[j][:], 0.0)
-        warm_in = sbuf("warm_in", [P, 8], F32)
-        warm_out = sbuf("warm_out", [P, 8], F32)
-        nc.gpsimd.memset(warm_in[:], 0.0)
-        nc.scalar.activation(out=warm_out[:], in_=warm_in[:], func=ACT.Tanh)
+            nc.gpsimd.memset(windows[j][:], 0.0)
+        neg_gate = sbuf("neg_gate", [P, PACK], F32)
+        nc.scalar.activation(out=neg_gate[:], in_=gate[:], func=ACT.Copy, scale=-1.0)
 
         c_woven = sbuf("c_woven", [P, N * PACK], BF16)
         c_places = c_woven[:].rearrange("p (n t) -> p t n", t=PACK)
-        for t in range(PACK):
+        for t in range(PACK - 1):
             nc.vector.tensor_copy(c_places[:, t, :], planes[t][:].indirect(offsets[:]))
+        for lo, hi in halves:
+            nc.vector.tensor_copy(c_places[:, PACK - 1, lo:hi],
+                                  planes[PACK - 1][:].indirect(offsets[:, lo // BAND : hi // BAND]))
         c_mx = operand("c", N)
-        quantize(c_mx, c_woven, E4M3, 0, N)
-        neg_gate = sbuf("neg_gate", [P, PACK], F32)
-        nc.vector.tensor_scalar(neg_gate[:], gate[:], -1.0, None, ALU.mult)
+        for lo, hi in halves:
+            quantize(c_mx, c_woven, E4M3, lo, hi)
 
-        qT_woven = sbuf("qT_woven", [P, R * PACK], BF16)
+        qT_woven = sbuf("dealt", [P, R * PACK], BF16)
         deal(nc.scalar.copy, qT_woven, raw["qT"], Q_SPLIT, P)
         deal(nc.vector.tensor_copy, qT_woven, raw["qT"], 0, Q_SPLIT)
         qT_mx = operand("qT", R)
@@ -92,7 +100,7 @@ def tile_attend_gat_tnh_c_kernel(tc, qT, cT, doT, rw, qm, dom, offs, out):
             product(bank, qT_mx, E4M3, t * P, c_mx, E4M3, True, True)
             scores.append(bank)
 
-        doT_woven = sbuf("doT_woven", [P, R * PACK], BF16)
+        doT_woven = sbuf("dealt", [P, R * PACK], BF16)
         deal(nc.vector.tensor_copy, doT_woven, raw["doT"], 0, P)
         doT_mx = operand("doT", R)
         dp = []
@@ -105,47 +113,55 @@ def tile_attend_gat_tnh_c_kernel(tc, qT, cT, doT, rw, qm, dom, offs, out):
         ds = sbuf("ds", [P, PACK, N], BF16)
         pw = sbuf("pw", [P, PACK, N], BF16)
         p = [sbuf("p%d" % t, [P, N], F32) for t in range(PACK)]
+        neg_sq = [sbuf("neg_sq%d" % t, [P, N], F32) for t in range(PACK)]
         for t in range(PACK):
-            p_sq = sbuf("p_sq%d" % t, [P, N], F32)
-            slope = sbuf("slope%d" % t, [P, N], F32)
             nc.scalar.activation(out=p[t][:], in_=scores[t][:], func=ACT.Tanh)
-            nc.scalar.activation(out=p_sq[:], in_=p[t][:], func=ACT.Square)
-            nc.vector.tensor_scalar(slope[:], p_sq[:], neg_gate[:, t : t + 1], gate[:, t : t + 1], ALU.mult, ALU.add)
-            if t < 3:
-                nc.vector.tensor_scalar(pw[:, t, :], p[t][:], gate[:, t : t + 1], None, ALU.mult)
-            else:
-                nc.scalar.activation(out=pw[:, t, :], in_=p[t][:], func=ACT.Copy, scale=gate[:, t : t + 1])
-            nc.vector.tensor_tensor(ds[:, t, :], dp[t][:], slope[:], ALU.mult)
+        for t in range(PACK):
+            nc.vector.scalar_tensor_tensor(neg_sq[t][:], p[t][:], neg_gate[:, t : t + 1], p[t][:], ALU.mult, ALU.mult)
+        for t in range(PACK):
+            nc.vector.scalar_tensor_tensor(ds[:, t, :], neg_sq[t][:], gate[:, t : t + 1], dp[t][:], ALU.add, ALU.mult)
+        for t in range(PACK):
+            nc.scalar.activation(out=pw[:, t, :], in_=p[t][:], func=ACT.Copy, scale=gate[:, t : t + 1])
 
         pw_woven = sbuf("pw_woven", [P, N * PACK], BF16)
         ds_woven = sbuf("ds_woven", [P, N * PACK], BF16)
-        qm_woven = sbuf("qm_woven", [P, D * PACK], BF16)
-        dom_woven = sbuf("dom_woven", [P, D * PACK], BF16)
         pw_mx = operand("pw", N)
         ds_mx = operand("ds", N)
-        qm_mx = operand("qm", D)
-        dom_mx = operand("dom", D)
 
-        weave(nc.scalar.copy, pw_woven, pw, 0, N)
-        weave(nc.vector.tensor_copy, ds_woven, ds, 0, N)
-        weave(nc.vector.tensor_copy, qm_woven, raw["qm"], 0, P)
-        weave(nc.vector.tensor_copy, dom_woven, raw["dom"], 0, P)
-        quantize(ds_mx, ds_woven, E5M2, 0, N)
-        quantize(qm_mx, qm_woven, E4M3, 0, P)
-        quantize(dom_mx, dom_woven, E5M2, 0, P)
-        quantize(pw_mx, pw_woven, E4M3, 0, N)
+        def feature_block(j):
+            woven = {}
+            for name in ("qm", "dom"):
+                woven[name] = sbuf(name + "_woven", [P, P * PACK], BF16)
+                weave(nc.scalar.copy, woven[name][:], raw[name][:, :, j * P : (j + 1) * P])
+            block = {}
+            for name, fmt in (("qm", E4M3), ("dom", E5M2)):
+                block[name] = operand(name + "%d" % j, P)
+                quantize(block[name], woven[name], fmt, 0, P)
+            return block
+
+        def along_rows(dst, woven, src, fmt, split):
+            weave(nc.scalar.copy, woven[:, PACK * split :], src[:, :, split:])
+            for lo, hi in ((0, N // 2), (N // 2, split)):
+                if lo < hi:
+                    weave(nc.vector.tensor_copy, woven[:, PACK * lo : PACK * hi], src[:, :, lo:hi])
+            for lo, hi in halves:
+                quantize(dst, woven, fmt, lo, hi)
+
+        along_rows(pw_mx, pw_woven, pw, E4M3, PW_SPLIT)
+        blocks = [feature_block(0)]
+        along_rows(ds_mx, ds_woven, ds, E5M2, DS_SPLIT)
+        blocks.append(feature_block(1))
 
         for j in range(D // P):
-            lo, hi = j * P, (j + 1) * P
             bank = psum.tile([P, N], F32, name="first%d" % j)
-            product(bank, qm_mx, E4M3, lo, ds_mx, E5M2, True, False)
-            product(bank, dom_mx, E5M2, lo, pw_mx, E4M3, False, True)
-            if hi < D:
-                weave(nc.scalar.copy, qm_woven, raw["qm"], hi, hi + P)
-                weave(nc.scalar.copy, dom_woven, raw["dom"], hi, hi + P)
-                quantize(qm_mx, qm_woven, E4M3, hi, hi + P)
-                quantize(dom_mx, dom_woven, E5M2, hi, hi + P)
+            product(bank, blocks[j]["dom"], E5M2, 0, pw_mx, E4M3, True, False)
+            product(bank, blocks[j]["qm"], E4M3, 0, ds_mx, E5M2, False, True)
             result = sbuf("result%d" % j, [P, N], F32)
-            nc.scalar.copy(out=result[:], in_=bank[:])
-            nc.vector.tensor_copy(windows[j][:].indirect(offsets[:]), result[:])
-            nc.sync.dma_start(out=out[lo:hi, :], in_=windows[j][:])
+            parts = halves if j < EVH else [(0, N)]
+            for lo, hi in parts:
+                nc.scalar.copy(out=result[:, lo:hi], in_=bank[:, lo:hi])
+            if j + 2 < D // P:
+                blocks.append(feature_block(j + 2))
+            for lo, hi in parts:
+                nc.vector.tensor_copy(windows[j][:].indirect(offsets[:, lo // BAND : hi // BAND]), result[:, lo:hi])
+            nc.sync.dma_start(out=out[j * P : (j + 1) * P, :], in_=windows[j][:])

@@ -73,8 +73,9 @@ def tile_attend_gat_tnh_c_kernel(tc, qT, cT, doT, rw, qm, dom, offs, out):
             nc.sync.dma_start(out=raw[name][:], in_=src[0].rearrange("(p j) w -> p j w", j=PACK))
 
         windows = [sbuf("window%d" % j, [P, T], F32) for j in range(D // P)]
-        for j in range(D // P):
-            nc.gpsimd.memset(windows[j][:], 0.0)
+        for j in range(D // P - 1):
+            nc.vector.memset(windows[j][:], 0.0)
+        nc.gpsimd.memset(windows[D // P - 1][:], 0.0)
         neg_gate = sbuf("neg_gate", [P, PACK], F32)
         nc.scalar.activation(out=neg_gate[:], in_=gate[:], func=ACT.Copy, scale=-1.0)
 

@@ -114,13 +114,13 @@ def tile_attend_gat_tnh_c_kernel(tc, qT, cT, doT, rw, qm, dom, offs, out):
         ds = sbuf("ds", [P, PACK, N], BF16)
         pw = sbuf("pw", [P, PACK, N], BF16)
         p = [sbuf("p%d" % t, [P, N], F32) for t in range(PACK)]
-        neg_sq = [sbuf("neg_sq%d" % t, [P, N], F32) for t in range(PACK)]
+        neg_sq = sbuf("doT_raw", [P, PACK, N], F32)
         for t in range(PACK):
             nc.scalar.activation(out=p[t][:], in_=scores[t][:], func=ACT.Tanh)
         for t in range(PACK):
-            nc.vector.scalar_tensor_tensor(neg_sq[t][:], p[t][:], neg_gate[:, t : t + 1], p[t][:], ALU.mult, ALU.mult)
+            nc.vector.scalar_tensor_tensor(neg_sq[:, t, :], p[t][:], neg_gate[:, t : t + 1], p[t][:], ALU.mult, ALU.mult)
         for t in range(PACK):
-            nc.vector.scalar_tensor_tensor(ds[:, t, :], neg_sq[t][:], gate[:, t : t + 1], dp[t][:], ALU.add, ALU.mult)
+            nc.vector.scalar_tensor_tensor(ds[:, t, :], neg_sq[:, t, :], gate[:, t : t + 1], dp[t][:], ALU.add, ALU.mult)
         for t in range(PACK):
             nc.scalar.activation(out=pw[:, t, :], in_=p[t][:], func=ACT.Copy, scale=gate[:, t : t + 1])
 

@@ -129,16 +129,17 @@ def tile_attend_gat_tnh_c_kernel(tc, qT, cT, doT, rw, qm, dom, offs, out):
         pw_mx = operand("pw", N)
         ds_mx = operand("ds", N)
 
-        def feature_block(j):
-            woven = {}
-            for name in ("qm", "dom"):
-                woven[name] = sbuf(name + "_woven", [P, P * PACK], BF16)
-                weave(nc.scalar.copy, woven[name][:], raw[name][:, :, j * P : (j + 1) * P])
+        def feature_block(j, copy, woven):
             block = {}
-            for name, fmt in (("qm", E4M3), ("dom", E5M2)):
+            for u, name in enumerate(("qm", "dom")):
+                weave(copy, woven[u], raw[name][:, :, j * P : (j + 1) * P])
+            for u, (name, fmt) in enumerate((("qm", E4M3), ("dom", E5M2))):
                 block[name] = operand(name + "%d" % j, P)
-                quantize(block[name], woven[name], fmt, 0, P)
+                quantize(block[name], woven[u], fmt, 0, P)
             return block
+
+        def block_buffers():
+            return [sbuf(name + "_woven", [P, P * PACK], BF16)[:] for name in ("qm", "dom")]
 
         def along_rows(dst, woven, src, fmt, split):
             weave(nc.scalar.copy, woven[:, PACK * split :], src[:, :, split:])
@@ -149,9 +150,9 @@ def tile_attend_gat_tnh_c_kernel(tc, qT, cT, doT, rw, qm, dom, offs, out):
                 quantize(dst, woven, fmt, lo, hi)
 
         along_rows(pw_mx, pw_woven, pw, E4M3, PW_SPLIT)
-        blocks = [feature_block(0)]
+        blocks = [feature_block(0, nc.scalar.copy, block_buffers())]
         along_rows(ds_mx, ds_woven, ds, E5M2, DS_SPLIT)
-        blocks.append(feature_block(1))
+        blocks.append(feature_block(1, nc.scalar.copy, block_buffers()))
 
         for j in range(D // P):
             bank = psum.tile([P, N], F32, name="first%d" % j)
@@ -161,8 +162,10 @@ def tile_attend_gat_tnh_c_kernel(tc, qT, cT, doT, rw, qm, dom, offs, out):
             parts = halves if j < EVH else [(0, N)]
             for lo, hi in parts:
                 nc.scalar.copy(out=result[:, lo:hi], in_=bank[:, lo:hi])
-            if j + 2 < D // P:
-                blocks.append(feature_block(j + 2))
+            if j == 0:
+                late = sbuf("ds_woven", [P, 2, P * PACK], BF16)
+                blocks.append(feature_block(2, nc.vector.tensor_copy, [late[:, 0, :], late[:, 1, :]]))
+                blocks.append(feature_block(3, nc.scalar.copy, block_buffers()))
             for lo, hi in parts:
                 nc.vector.tensor_copy(windows[j][:].indirect(offsets[:, lo // BAND : hi // BAND]), result[:, lo:hi])
             nc.sync.dma_start(out=out[j * P : (j + 1) * P, :], in_=windows[j][:])

@@ -19,10 +19,7 @@ P = 128
 PACK = 4
 BAND = 16
 RUN = 4
-Q_SPLIT = 80
-PW_SPLIT = 256
-DS_SPLIT = 256
-EVH = 0
+DS_SPLIT = 192
 
 
 def tile_attend_gat_tnh_c_kernel(tc, qT, cT, doT, rw, qm, dom, offs, out):
@@ -53,8 +50,8 @@ def tile_attend_gat_tnh_c_kernel(tc, qT, cT, doT, rw, qm, dom, offs, out):
                  in_=src.rearrange("p t (c i) -> p c t i", i=RUN))
 
         def deal(copy, dst, src, lo, hi):
-            copy(out=dst[:].rearrange("p (t s j) -> p s j t", t=PACK, j=PACK)[:, lo:hi],
-                 in_=src[:].rearrange("p j (s t) -> p s j t", t=PACK)[:, lo:hi])
+            copy(out=dst[:].rearrange("p (t s j) -> p s j t", t=PACK, j=PACK)[:, :, :, lo:hi],
+                 in_=src[:].rearrange("p j (s t) -> p s j t", t=PACK)[:, :, :, lo:hi])
 
         halves = [(0, N // 2), (N // 2, N)]
 
@@ -67,17 +64,32 @@ def tile_attend_gat_tnh_c_kernel(tc, qT, cT, doT, rw, qm, dom, offs, out):
             nc.sync.dma_start(out=planes[t][:], in_=c_rows[t])
         gate = sbuf("gate", [P, PACK], F32)
         nc.scalar.dma_start(out=gate[:], in_=rw[0].rearrange("(p t) o -> p (t o)", t=PACK))
-        raw = {}
-        for name, src in (("qT", qT), ("doT", doT), ("dom", dom), ("qm", qm)):
-            raw[name] = sbuf(name + "_raw", [P, PACK, 512], F32)
-            nc.sync.dma_start(out=raw[name][:], in_=src[0].rearrange("(p j) w -> p j w", j=PACK))
+
+        def load(name, src, lo, hi):
+            tile = sbuf(name, [P, PACK, hi - lo], F32)
+            nc.sync.dma_start(out=tile[:], in_=src[0].rearrange("(p j) w -> p j w", j=PACK)[:, :, lo:hi])
+            return tile
+
+        q_raw = load("qT_raw", qT, 0, R)
+        do_raw = load("doT_raw", doT, 0, R)
+        raw = {"dom": load("dom_raw", dom, 0, D), "qm": load("qm_raw", qm, 0, D)}
 
         windows = [sbuf("window%d" % j, [P, T], F32) for j in range(D // P)]
         for j in range(D // P - 1):
             nc.vector.memset(windows[j][:], 0.0)
         nc.gpsimd.memset(windows[D // P - 1][:], 0.0)
-        neg_gate = sbuf("neg_gate", [P, PACK], F32)
-        nc.scalar.activation(out=neg_gate[:], in_=gate[:], func=ACT.Copy, scale=-1.0)
+        size = sbuf("size", [P, PACK], F32)
+        nc.scalar.activation(out=size[:], in_=gate[:], func=ACT.Abs)
+        half = sbuf("half", [P, PACK], F32)
+        nc.gpsimd.memset(half[:], 0.5)
+        root = sbuf("root", [P, PACK], F32)
+        nc.gpsimd.tensor_tensor(root[:], size[:], half[:], ALU.pow)
+        level = sbuf("level", [P, PACK], F32)
+        nc.gpsimd.tensor_tensor(level[:], root[:], root[:], ALU.mult)
+        below = sbuf("below", [P, PACK], F32)
+        nc.gpsimd.tensor_scalar(below[:], gate[:], 0.0, 2.0, ALU.is_lt, ALU.mult)
+        flip = sbuf("flip", [P, PACK], F32)
+        nc.gpsimd.tensor_scalar(flip[:], below[:], 1.0, -1.0, ALU.mult, ALU.add)
 
         c_woven = sbuf("c_woven", [P, N * PACK], BF16)
         c_places = c_woven[:].rearrange("p (n t) -> p t n", t=PACK)
@@ -90,82 +102,122 @@ def tile_attend_gat_tnh_c_kernel(tc, qT, cT, doT, rw, qm, dom, offs, out):
         for lo, hi in halves:
             quantize(c_mx, c_woven, E4M3, lo, hi)
 
-        qT_woven = sbuf("dealt", [P, R * PACK], BF16)
-        deal(nc.scalar.copy, qT_woven, raw["qT"], Q_SPLIT, P)
-        deal(nc.vector.tensor_copy, qT_woven, raw["qT"], 0, Q_SPLIT)
+        q_dealt = sbuf("dealt", [P, R * PACK], BF16)
+        deal(nc.vector.tensor_copy, q_dealt, q_raw, 0, 2)
+        deal(nc.scalar.copy, q_dealt, q_raw, 2, 4)
         qT_mx = operand("qT", R)
         scores = []
         for t in range(PACK):
-            quantize(qT_mx, qT_woven, E4M3, t * P, (t + 1) * P)
+            quantize(qT_mx, q_dealt, E4M3, t * P, (t + 1) * P)
             bank = psum.tile([P, N], F32, name="first%d" % t)
             product(bank, qT_mx, E4M3, t * P, c_mx, E4M3, True, True)
             scores.append(bank)
 
-        doT_woven = sbuf("dealt", [P, R * PACK], BF16)
-        deal(nc.vector.tensor_copy, doT_woven, raw["doT"], 0, P)
-        doT_mx = operand("doT", R)
-        dp = []
-        for t in range(PACK):
-            quantize(doT_mx, doT_woven, E5M2, t * P, (t + 1) * P)
-            bank = psum.tile([P, N], F32, name="second%d" % t)
-            product(bank, doT_mx, E5M2, t * P, c_mx, E4M3, True, True)
-            dp.append(bank)
-
+        do_dealt = sbuf("dealt", [P, R * PACK], BF16)
+        deal(nc.vector.tensor_copy, do_dealt, do_raw, 0, 2)
+        deal(nc.vector.tensor_copy, do_dealt, do_raw, 2, 4)
         ds = sbuf("ds", [P, PACK, N], BF16)
-        pw = sbuf("pw", [P, PACK, N], BF16)
+        pw = sbuf("doT_raw", [P, PACK, N], BF16)
+        pw_woven = sbuf("pw_woven", [P, N * PACK], BF16)
         p = [sbuf("p%d" % t, [P, N], F32) for t in range(PACK)]
-        neg_sq = sbuf("doT_raw", [P, PACK, N], F32)
+        sq = [sbuf("sq%d" % t, [P, N], F32) for t in range(PACK)]
         for t in range(PACK):
             nc.scalar.activation(out=p[t][:], in_=scores[t][:], func=ACT.Tanh)
         for t in range(PACK):
-            nc.vector.scalar_tensor_tensor(neg_sq[:, t, :], p[t][:], neg_gate[:, t : t + 1], p[t][:], ALU.mult, ALU.mult)
-        for t in range(PACK):
-            nc.vector.scalar_tensor_tensor(ds[:, t, :], neg_sq[:, t, :], gate[:, t : t + 1], dp[t][:], ALU.add, ALU.mult)
-        for t in range(PACK):
-            nc.scalar.activation(out=pw[:, t, :], in_=p[t][:], func=ACT.Copy, scale=gate[:, t : t + 1])
+            nc.scalar.activation(out=sq[t][:], in_=p[t][:], func=ACT.Square, scale=root[:, t : t + 1])
 
-        pw_woven = sbuf("pw_woven", [P, N * PACK], BF16)
+        def weave_slots(copy, dst, src, lo, hi):
+            weave(copy, dst[:, PACK * lo : PACK * hi], src[:, :, lo:hi])
+
+        def gated(t):
+            nc.vector.tensor_scalar(pw[:, t, :], p[t][:], gate[:, t : t + 1], None, ALU.mult)
+
+        def slope(t):
+            nc.vector.scalar_tensor_tensor(ds[:, t, :], sq[t][:], level[:, t : t + 1], dp[t][:], ALU.subtract, ALU.mult)
+
+        doT_mx = operand("doT", R)
+        dp = []
+        for t in range(PACK):
+            quantize(doT_mx, do_dealt, E5M2, t * P, (t + 1) * P)
+            bank = psum.tile([P, N], F32, name="second%d" % t)
+            product(bank, doT_mx, E5M2, t * P, c_mx, E4M3, True, True)
+            dp.append(bank)
+        for t in range(PACK):
+            gated(t)
+        slope(0)
+        weave_slots(nc.vector.tensor_copy, pw_woven, pw, 0, N // 2)
+        for t in range(1, PACK):
+            slope(t)
+
         ds_woven = sbuf("ds_woven", [P, N * PACK], BF16)
         pw_mx = operand("pw", N)
         ds_mx = operand("ds", N)
+        rows = {}
+        woven = {}
+        codes = {}
 
-        def feature_block(j, copy, woven):
-            block = {}
-            for u, name in enumerate(("qm", "dom")):
-                weave(copy, woven[u], raw[name][:, :, j * P : (j + 1) * P])
-            for u, (name, fmt) in enumerate((("qm", E4M3), ("dom", E5M2))):
-                block[name] = operand(name + "%d" % j, P)
-                quantize(block[name], woven[u], fmt, 0, P)
-            return block
+        def flip_qm(blocks, tag):
+            width = len(blocks) * P
+            flipped = sbuf(tag, [P, PACK, width], BF16)
+            for t in range(PACK):
+                nc.vector.tensor_scalar(flipped[:, t, :], raw["qm"][:, t, blocks[0] * P : blocks[0] * P + width],
+                                        flip[:, t : t + 1], None, ALU.mult)
+            for u, j in enumerate(blocks):
+                rows["qm", j] = flipped[:, :, u * P : (u + 1) * P]
 
-        def block_buffers():
-            return [sbuf(name + "_woven", [P, P * PACK], BF16)[:] for name in ("qm", "dom")]
+        for j in range(D // P):
+            rows["dom", j] = raw["dom"][:, :, j * P : (j + 1) * P]
 
-        def along_rows(dst, woven, src, fmt, split):
-            weave(nc.scalar.copy, woven[:, PACK * split :], src[:, :, split:])
-            for lo, hi in ((0, N // 2), (N // 2, split)):
-                if lo < hi:
-                    weave(nc.vector.tensor_copy, woven[:, PACK * lo : PACK * hi], src[:, :, lo:hi])
-            for lo, hi in halves:
-                quantize(dst, woven, fmt, lo, hi)
+        def weave_block(name, j, copy, buffer):
+            woven[name, j] = buffer
+            weave(copy, buffer, rows[name, j])
 
-        along_rows(pw_mx, pw_woven, pw, E4M3, PW_SPLIT)
-        blocks = [feature_block(0, nc.scalar.copy, block_buffers())]
-        along_rows(ds_mx, ds_woven, ds, E5M2, DS_SPLIT)
-        blocks.append(feature_block(1, nc.scalar.copy, block_buffers()))
+        def weave_blocks(j, tag):
+            tile = sbuf(tag, [P, 2, P * PACK], BF16)
+            for u, name in enumerate(("dom", "qm")):
+                weave_block(name, j, nc.scalar.copy, tile[:, u, :])
+
+        def quantize_block(name, j):
+            codes[name, j] = operand("%s%d" % (name, j), P)
+            quantize(codes[name, j], woven[name, j], E4M3 if name == "qm" else E5M2, 0, P)
+
+        flip_qm([0, 1], "flipped")
+        first = sbuf("first_woven", [P, 2, P * PACK], BF16)
+        weave_block("dom", 0, nc.scalar.copy, first[:, 0, :])
+        weave_slots(nc.scalar.copy, pw_woven, pw, N // 2, N)
+        weave_block("qm", 0, nc.scalar.copy, first[:, 1, :])
+        weave_slots(nc.scalar.copy, ds_woven, ds, DS_SPLIT, N // 2)
+        weave_slots(nc.scalar.copy, ds_woven, ds, N // 2, N)
+        quantize(pw_mx, pw_woven, E4M3, 0, N // 2)
+        weave_slots(nc.vector.tensor_copy, ds_woven, ds, 0, DS_SPLIT)
+        quantize_block("dom", 0)
+        quantize(pw_mx, pw_woven, E4M3, N // 2, N)
+        quantize(ds_mx, ds_woven, E5M2, 0, N // 2)
+        quantize_block("qm", 0)
+        quantize(ds_mx, ds_woven, E5M2, N // 2, N)
+        weave_blocks(1, "ds")
+        flip_qm([2, 3], "ds_woven")
+        quantize_block("dom", 1)
+        quantize_block("qm", 1)
 
         for j in range(D // P):
             bank = psum.tile([P, N], F32, name="first%d" % j)
-            product(bank, blocks[j]["dom"], E5M2, 0, pw_mx, E4M3, True, False)
-            product(bank, blocks[j]["qm"], E4M3, 0, ds_mx, E5M2, False, True)
+            product(bank, codes["dom", j], E5M2, 0, pw_mx, E4M3, True, False)
+            product(bank, codes["qm", j], E4M3, 0, ds_mx, E5M2, False, True)
             result = sbuf("result%d" % j, [P, N], F32)
-            parts = halves if j < EVH else [(0, N)]
+            parts = halves if j == 0 else [(0, N)]
             for lo, hi in parts:
                 nc.scalar.copy(out=result[:, lo:hi], in_=bank[:, lo:hi])
             if j == 0:
-                late = sbuf("ds_woven", [P, 2, P * PACK], BF16)
-                blocks.append(feature_block(2, nc.vector.tensor_copy, [late[:, 0, :], late[:, 1, :]]))
-                blocks.append(feature_block(3, nc.scalar.copy, block_buffers()))
+                weave_blocks(2, "ds")
+            if j == 1:
+                weave_blocks(3, "ds")
             for lo, hi in parts:
                 nc.vector.tensor_copy(windows[j][:].indirect(offsets[:, lo // BAND : hi // BAND]), result[:, lo:hi])
             nc.sync.dma_start(out=out[j * P : (j + 1) * P, :], in_=windows[j][:])
+            if j == 0:
+                quantize_block("dom", 2)
+                quantize_block("qm", 2)
+            if j == 1:
+                quantize_block("dom", 3)
+                quantize_block("qm", 3)

@@ -165,6 +165,13 @@ def tile_attend_gat_tnh_c_kernel(tc, qT, cT, doT, rw, qm, dom, offs, out):
             for u, j in enumerate(blocks):
                 rows["qm", j] = flipped[:, :, u * P : (u + 1) * P]
 
+        def flip_last():
+            flipped = sbuf("ds_woven", [P, PACK, P], BF16)
+            for t in range(PACK):
+                nc.scalar.activation(out=flipped[:, t, :], in_=raw["qm"][:, t, D - P :], func=ACT.Copy,
+                                     scale=flip[:, t : t + 1])
+            rows["qm", D // P - 1] = flipped[:]
+
         for j in range(D // P):
             rows["dom", j] = raw["dom"][:, :, j * P : (j + 1) * P]
 
@@ -172,16 +179,16 @@ def tile_attend_gat_tnh_c_kernel(tc, qT, cT, doT, rw, qm, dom, offs, out):
             woven[name, j] = buffer
             weave(copy, buffer, rows[name, j])
 
-        def weave_blocks(j, tag):
+        def weave_blocks(j, copy, tag):
             tile = sbuf(tag, [P, 2, P * PACK], BF16)
             for u, name in enumerate(("dom", "qm")):
-                weave_block(name, j, nc.scalar.copy, tile[:, u, :])
+                weave_block(name, j, copy, tile[:, u, :])
 
         def quantize_block(name, j):
             codes[name, j] = operand("%s%d" % (name, j), P)
             quantize(codes[name, j], woven[name, j], E4M3 if name == "qm" else E5M2, 0, P)
 
-        flip_qm([0, 1], "flipped")
+        flip_qm([0, 1, 2], "flipped")
         first = sbuf("first_woven", [P, 2, P * PACK], BF16)
         weave_block("dom", 0, nc.scalar.copy, first[:, 0, :])
         weave_slots(nc.scalar.copy, pw_woven, pw, N // 2, N)
@@ -195,29 +202,26 @@ def tile_attend_gat_tnh_c_kernel(tc, qT, cT, doT, rw, qm, dom, offs, out):
         quantize(ds_mx, ds_woven, E5M2, 0, N // 2)
         quantize_block("qm", 0)
         quantize(ds_mx, ds_woven, E5M2, N // 2, N)
-        weave_blocks(1, "ds")
-        flip_qm([2, 3], "ds_woven")
-        quantize_block("dom", 1)
-        quantize_block("qm", 1)
+        weave_blocks(2, nc.scalar.copy, "ds")
+        weave_blocks(1, nc.vector.tensor_copy, "ds_woven")
+        for j in (1, 2):
+            quantize_block("dom", j)
+            quantize_block("qm", j)
 
         for j in range(D // P):
             bank = psum.tile([P, N], F32, name="first%d" % j)
             product(bank, codes["dom", j], E5M2, 0, pw_mx, E4M3, True, False)
             product(bank, codes["qm", j], E4M3, 0, ds_mx, E5M2, False, True)
-            result = sbuf("result%d" % j, [P, N], F32)
+            result = sbuf("ds_woven" if j == 2 else "result%d" % j, [P, N], F32)
             parts = halves if j == 0 else [(0, N)]
             for lo, hi in parts:
                 nc.scalar.copy(out=result[:, lo:hi], in_=bank[:, lo:hi])
-            if j == 0:
-                weave_blocks(2, "ds")
             if j == 1:
-                weave_blocks(3, "ds")
+                flip_last()
+                weave_blocks(3, nc.scalar.copy, "ds")
             for lo, hi in parts:
                 nc.vector.tensor_copy(windows[j][:].indirect(offsets[:, lo // BAND : hi // BAND]), result[:, lo:hi])
             nc.sync.dma_start(out=out[j * P : (j + 1) * P, :], in_=windows[j][:])
-            if j == 0:
-                quantize_block("dom", 2)
-                quantize_block("qm", 2)
             if j == 1:
                 quantize_block("dom", 3)
                 quantize_block("qm", 3)

@@ -114,8 +114,7 @@ def tile_attend_gat_tnh_c_kernel(tc, qT, cT, doT, rw, qm, dom, offs, out):
             scores.append(bank)
 
         do_dealt = sbuf("dealt", [P, R * PACK], BF16)
-        deal(nc.vector.tensor_copy, do_dealt, do_raw, 0, 2)
-        deal(nc.vector.tensor_copy, do_dealt, do_raw, 2, 4)
+        deal(nc.vector.tensor_copy, do_dealt, do_raw, 0, PACK)
         ds = sbuf("ds", [P, PACK, N], BF16)
         pw = sbuf("doT_raw", [P, PACK, N], BF16)
         pw_woven = sbuf("pw_woven", [P, N * PACK], BF16)

@@ -19,7 +19,7 @@ P = 128
 PACK = 4
 BAND = 16
 RUN = 4
-DS_SPLIT = 192
+DS_SPLIT = 256
 
 
 def tile_attend_gat_tnh_c_kernel(tc, qT, cT, doT, rw, qm, dom, offs, out):
@@ -49,9 +49,9 @@ def tile_attend_gat_tnh_c_kernel(tc, qT, cT, doT, rw, qm, dom, offs, out):
             copy(out=dst.rearrange("p (c i t) -> p c t i", i=RUN, t=PACK),
                  in_=src.rearrange("p t (c i) -> p c t i", i=RUN))
 
-        def deal(copy, dst, src, lo, hi):
-            copy(out=dst[:].rearrange("p (t s j) -> p s j t", t=PACK, j=PACK)[:, :, :, lo:hi],
-                 in_=src[:].rearrange("p j (s t) -> p s j t", t=PACK)[:, :, :, lo:hi])
+        def deal(copy, dst, src, rows, places):
+            copy(out=dst[:].rearrange("p (t s j) -> p s j t", t=PACK, j=PACK)[:, :, rows[0] : rows[1], places[0] : places[1]],
+                 in_=src.rearrange("p j (s t) -> p s j t", t=PACK)[:, :, :, places[0] : places[1]])
 
         halves = [(0, N // 2), (N // 2, N)]
 
@@ -66,13 +66,13 @@ def tile_attend_gat_tnh_c_kernel(tc, qT, cT, doT, rw, qm, dom, offs, out):
         nc.scalar.dma_start(out=gate[:], in_=rw[0].rearrange("(p t) o -> p (t o)", t=PACK))
 
         def load(name, src, lo, hi):
-            tile = sbuf(name, [P, PACK, hi - lo], F32)
-            nc.sync.dma_start(out=tile[:], in_=src[0].rearrange("(p j) w -> p j w", j=PACK)[:, :, lo:hi])
+            tile = sbuf(name, [P, hi - lo, src.shape[2]], F32)
+            nc.sync.dma_start(out=tile[:], in_=src[0].rearrange("(p j) w -> p j w", j=PACK)[:, lo:hi, :])
             return tile
 
-        q_raw = load("qT_raw", qT, 0, R)
-        do_raw = load("doT_raw", doT, 0, R)
-        raw = {"dom": load("dom_raw", dom, 0, D), "qm": load("qm_raw", qm, 0, D)}
+        q_raw = [load("qT_raw%d" % h, qT, 2 * h, 2 * h + 2) for h in range(2)]
+        do_raw = [load("doT_raw%d" % h, doT, 2 * h, 2 * h + 2) for h in range(2)]
+        raw = {"dom": load("dom_raw", dom, 0, PACK), "qm": load("qm_raw", qm, 0, PACK)}
 
         windows = [sbuf("window%d" % j, [P, T], F32) for j in range(D // P)]
         for j in range(D // P - 1):
@@ -102,9 +102,11 @@ def tile_attend_gat_tnh_c_kernel(tc, qT, cT, doT, rw, qm, dom, offs, out):
         for lo, hi in halves:
             quantize(c_mx, c_woven, E4M3, lo, hi)
 
-        q_dealt = sbuf("dealt", [P, R * PACK], BF16)
-        deal(nc.vector.tensor_copy, q_dealt, q_raw, 0, 2)
-        deal(nc.scalar.copy, q_dealt, q_raw, 2, 4)
+        q_dealt = sbuf("q_dealt", [P, R * PACK], BF16)
+        for places in ((0, 2), (2, 4)):
+            deal(nc.scalar.copy, q_dealt, q_raw[0][:], (0, 2), places)
+        for places in ((0, 2), (2, 4)):
+            deal(nc.vector.tensor_copy, q_dealt, q_raw[1][:], (2, 4), places)
         qT_mx = operand("qT", R)
         scores = []
         for t in range(PACK):
@@ -113,10 +115,11 @@ def tile_attend_gat_tnh_c_kernel(tc, qT, cT, doT, rw, qm, dom, offs, out):
             product(bank, qT_mx, E4M3, t * P, c_mx, E4M3, True, True)
             scores.append(bank)
 
-        do_dealt = sbuf("dealt", [P, R * PACK], BF16)
-        deal(nc.vector.tensor_copy, do_dealt, do_raw, 0, PACK)
+        do_dealt = sbuf("q_dealt", [P, R * PACK], BF16)
+        for h in range(2):
+            deal(nc.vector.tensor_copy, do_dealt, do_raw[h][:], (2 * h, 2 * h + 2), (0, PACK))
         ds = sbuf("ds", [P, PACK, N], BF16)
-        pw = sbuf("doT_raw", [P, PACK, N], BF16)
+        pw = sbuf("doT_raw1", [P, PACK, N], BF16)
         pw_woven = sbuf("pw_woven", [P, N * PACK], BF16)
         p = [sbuf("p%d" % t, [P, N], F32) for t in range(PACK)]
         sq = [sbuf("sq%d" % t, [P, N], F32) for t in range(PACK)]
@@ -164,36 +167,40 @@ def tile_attend_gat_tnh_c_kernel(tc, qT, cT, doT, rw, qm, dom, offs, out):
             for u, j in enumerate(blocks):
                 rows["qm", j] = flipped[:, :, u * P : (u + 1) * P]
 
-        def flip_last():
-            flipped = sbuf("ds_woven", [P, PACK, P], BF16)
-            for t in range(PACK):
-                nc.scalar.activation(out=flipped[:, t, :], in_=raw["qm"][:, t, D - P :], func=ACT.Copy,
-                                     scale=flip[:, t : t + 1])
-            rows["qm", D // P - 1] = flipped[:]
-
         for j in range(D // P):
             rows["dom", j] = raw["dom"][:, :, j * P : (j + 1) * P]
 
-        def weave_block(name, j, copy, buffer):
-            woven[name, j] = buffer
-            weave(copy, buffer, rows[name, j])
-
-        def weave_blocks(j, copy, tag):
-            tile = sbuf(tag, [P, 2, P * PACK], BF16)
-            for u, name in enumerate(("dom", "qm")):
-                weave_block(name, j, copy, tile[:, u, :])
+        def weave_block(name, j, copy, tag):
+            woven[name, j] = sbuf(tag, [P, P * PACK], BF16)[:]
+            weave(copy, woven[name, j], rows[name, j])
 
         def quantize_block(name, j):
             codes[name, j] = operand("%s%d" % (name, j), P)
             quantize(codes[name, j], woven[name, j], E4M3 if name == "qm" else E5M2, 0, P)
 
-        flip_qm([0, 1, 2], "flipped")
-        first = sbuf("first_woven", [P, 2, P * PACK], BF16)
-        weave_block("dom", 0, nc.scalar.copy, first[:, 0, :])
+        banks = {}
+        results = {}
+
+        def products(j):
+            banks[j] = psum.tile([P, N], F32, name="first%d" % j)
+            product(banks[j], codes["dom", j], E5M2, 0, pw_mx, E4M3, True, False)
+            product(banks[j], codes["qm", j], E4M3, 0, ds_mx, E5M2, False, True)
+            results[j] = sbuf("result%d" % j, [P, N], F32)
+
+        def empty(j, lo, hi):
+            nc.scalar.copy(out=results[j][:, lo:hi], in_=banks[j][:, lo:hi])
+
+        def scatter(j, lo, hi):
+            nc.vector.tensor_copy(windows[j][:].indirect(offsets[:, lo // BAND : hi // BAND]), results[j][:, lo:hi])
+
+        def store(j):
+            nc.sync.dma_start(out=out[j * P : (j + 1) * P, :], in_=windows[j][:])
+
+        flip_qm([0], "flipped0")
+        weave_block("dom", 0, nc.scalar.copy, "dom_woven0")
         weave_slots(nc.scalar.copy, pw_woven, pw, N // 2, N)
-        weave_block("qm", 0, nc.scalar.copy, first[:, 1, :])
-        weave_slots(nc.scalar.copy, ds_woven, ds, DS_SPLIT, N // 2)
-        weave_slots(nc.scalar.copy, ds_woven, ds, N // 2, N)
+        weave_block("qm", 0, nc.scalar.copy, "qm_woven0")
+        weave_slots(nc.scalar.copy, ds_woven, ds, DS_SPLIT, N)
         quantize(pw_mx, pw_woven, E4M3, 0, N // 2)
         weave_slots(nc.vector.tensor_copy, ds_woven, ds, 0, DS_SPLIT)
         quantize_block("dom", 0)
@@ -201,26 +208,36 @@ def tile_attend_gat_tnh_c_kernel(tc, qT, cT, doT, rw, qm, dom, offs, out):
         quantize(ds_mx, ds_woven, E5M2, 0, N // 2)
         quantize_block("qm", 0)
         quantize(ds_mx, ds_woven, E5M2, N // 2, N)
-        weave_blocks(2, nc.scalar.copy, "ds")
-        weave_blocks(1, nc.vector.tensor_copy, "ds_woven")
-        for j in (1, 2):
-            quantize_block("dom", j)
-            quantize_block("qm", j)
+        products(0)
 
-        for j in range(D // P):
-            bank = psum.tile([P, N], F32, name="first%d" % j)
-            product(bank, codes["dom", j], E5M2, 0, pw_mx, E4M3, True, False)
-            product(bank, codes["qm", j], E4M3, 0, ds_mx, E5M2, False, True)
-            result = sbuf("ds_woven" if j == 2 else "result%d" % j, [P, N], F32)
-            parts = halves if j == 0 else [(0, N)]
-            for lo, hi in parts:
-                nc.scalar.copy(out=result[:, lo:hi], in_=bank[:, lo:hi])
-            if j == 1:
-                flip_last()
-                weave_blocks(3, nc.scalar.copy, "ds")
-            for lo, hi in parts:
-                nc.vector.tensor_copy(windows[j][:].indirect(offsets[:, lo // BAND : hi // BAND]), result[:, lo:hi])
-            nc.sync.dma_start(out=out[j * P : (j + 1) * P, :], in_=windows[j][:])
-            if j == 1:
-                quantize_block("dom", 3)
-                quantize_block("qm", 3)
+        pair = sbuf("ds", [P, 2, P * PACK], BF16)
+        for u in range(2):
+            woven["dom", 1 + u] = pair[:, u, :]
+            weave(nc.scalar.copy, pair[:, u, :], rows["dom", 1 + u])
+        flip_qm([1, 2], "ds_woven")
+        weave_block("qm", 1, nc.vector.tensor_copy, "pw_woven")
+        quantize_block("dom", 1)
+        quantize_block("dom", 2)
+        quantize_block("qm", 1)
+        products(1)
+        for lo, hi in halves:
+            empty(0, lo, hi)
+        weave_block("qm", 2, nc.scalar.copy, "ds")
+        for lo, hi in halves:
+            scatter(0, lo, hi)
+        store(0)
+        quantize_block("qm", 2)
+        products(2)
+        flip_qm([3], "result0")
+        empty(1, 0, N)
+        weave_block("dom", 3, nc.scalar.copy, "ds_woven")
+        weave_block("qm", 3, nc.scalar.copy, "ds")
+        scatter(1, 0, N)
+        store(1)
+        quantize_block("dom", 3)
+        quantize_block("qm", 3)
+        products(3)
+        for j in (2, 3):
+            empty(j, 0, N)
+            scatter(j, 0, N)
+            store(j)

@@ -19,7 +19,7 @@ P = 128
 PACK = 4
 BAND = 16
 RUN = 4
-DS_SPLIT = 256
+DS_SPLIT = 192
 
 
 def tile_attend_gat_tnh_c_kernel(tc, qT, cT, doT, rw, qm, dom, offs, out):
@@ -70,8 +70,8 @@ def tile_attend_gat_tnh_c_kernel(tc, qT, cT, doT, rw, qm, dom, offs, out):
             nc.sync.dma_start(out=tile[:], in_=src[0].rearrange("(p j) w -> p j w", j=PACK)[:, lo:hi, :])
             return tile
 
-        q_raw = [load("qT_raw%d" % h, qT, 2 * h, 2 * h + 2) for h in range(2)]
-        do_raw = [load("doT_raw%d" % h, doT, 2 * h, 2 * h + 2) for h in range(2)]
+        q_raw = load("qT_raw", qT, 0, PACK)
+        do_raw = load("doT_raw", doT, 0, PACK)
         raw = {"dom": load("dom_raw", dom, 0, PACK), "qm": load("qm_raw", qm, 0, PACK)}
 
         windows = [sbuf("window%d" % j, [P, T], F32) for j in range(D // P)]
@@ -103,10 +103,8 @@ def tile_attend_gat_tnh_c_kernel(tc, qT, cT, doT, rw, qm, dom, offs, out):
             quantize(c_mx, c_woven, E4M3, lo, hi)
 
         q_dealt = sbuf("q_dealt", [P, R * PACK], BF16)
-        for places in ((0, 2), (2, 4)):
-            deal(nc.scalar.copy, q_dealt, q_raw[0][:], (0, 2), places)
-        for places in ((0, 2), (2, 4)):
-            deal(nc.vector.tensor_copy, q_dealt, q_raw[1][:], (2, 4), places)
+        deal(nc.vector.tensor_copy, q_dealt, q_raw[:], (0, PACK), (0, 2))
+        deal(nc.scalar.copy, q_dealt, q_raw[:], (0, PACK), (2, 4))
         qT_mx = operand("qT", R)
         scores = []
         for t in range(PACK):
@@ -116,10 +114,9 @@ def tile_attend_gat_tnh_c_kernel(tc, qT, cT, doT, rw, qm, dom, offs, out):
             scores.append(bank)
 
         do_dealt = sbuf("q_dealt", [P, R * PACK], BF16)
-        for h in range(2):
-            deal(nc.vector.tensor_copy, do_dealt, do_raw[h][:], (2 * h, 2 * h + 2), (0, PACK))
+        deal(nc.vector.tensor_copy, do_dealt, do_raw[:], (0, PACK), (0, PACK))
         ds = sbuf("ds", [P, PACK, N], BF16)
-        pw = sbuf("doT_raw1", [P, PACK, N], BF16)
+        pw = sbuf("doT_raw", [P, PACK, N], BF16)
         pw_woven = sbuf("pw_woven", [P, N * PACK], BF16)
         p = [sbuf("p%d" % t, [P, N], F32) for t in range(PACK)]
         sq = [sbuf("sq%d" % t, [P, N], F32) for t in range(PACK)]

@@ -20,6 +20,7 @@ PACK = 4
 BAND = 16
 RUN = 4
 DS_SPLIT = 192
+PW_SPLIT = 384
 
 
 def tile_attend_gat_tnh_c_kernel(tc, qT, cT, doT, rw, qm, dom, offs, out):
@@ -136,16 +137,17 @@ def tile_attend_gat_tnh_c_kernel(tc, qT, cT, doT, rw, qm, dom, offs, out):
 
         doT_mx = operand("doT", R)
         dp = []
+        gated(0)
         for t in range(PACK):
             quantize(doT_mx, do_dealt, E5M2, t * P, (t + 1) * P)
             bank = psum.tile([P, N], F32, name="second%d" % t)
             product(bank, doT_mx, E5M2, t * P, c_mx, E4M3, True, True)
             dp.append(bank)
-        for t in range(PACK):
-            gated(t)
-        slope(0)
-        weave_slots(nc.vector.tensor_copy, pw_woven, pw, 0, N // 2)
         for t in range(1, PACK):
+            gated(t)
+        nc.gpsimd.tensor_scalar(pw_woven[:, : PACK * PW_SPLIT].rearrange("p (n t) -> p n t", t=PACK),
+                                pw[:, :, :PW_SPLIT].rearrange("p t n -> p n t"), 1.0, 0.0, ALU.mult, ALU.add)
+        for t in range(PACK):
             slope(t)
 
         ds_woven = sbuf("ds_woven", [P, N * PACK], BF16)
@@ -155,14 +157,12 @@ def tile_attend_gat_tnh_c_kernel(tc, qT, cT, doT, rw, qm, dom, offs, out):
         woven = {}
         codes = {}
 
-        def flip_qm(blocks, tag):
-            width = len(blocks) * P
-            flipped = sbuf(tag, [P, PACK, width], BF16)
+        def flip_qm(first, last, flipped):
             for t in range(PACK):
-                nc.vector.tensor_scalar(flipped[:, t, :], raw["qm"][:, t, blocks[0] * P : blocks[0] * P + width],
+                nc.vector.tensor_scalar(flipped[:, t, :], raw["qm"][:, t, first * P : (last + 1) * P],
                                         flip[:, t : t + 1], None, ALU.mult)
-            for u, j in enumerate(blocks):
-                rows["qm", j] = flipped[:, :, u * P : (u + 1) * P]
+            for j in range(first, last + 1):
+                rows["qm", j] = flipped[:, :, (j - first) * P : (j - first + 1) * P]
 
         for j in range(D // P):
             rows["dom", j] = raw["dom"][:, :, j * P : (j + 1) * P]
@@ -178,63 +178,58 @@ def tile_attend_gat_tnh_c_kernel(tc, qT, cT, doT, rw, qm, dom, offs, out):
         banks = {}
         results = {}
 
-        def products(j):
+        def products(j, first, second):
+            moving = {"dom": (E5M2, pw_mx, E4M3), "qm": (E4M3, ds_mx, E5M2)}
             banks[j] = psum.tile([P, N], F32, name="first%d" % j)
-            product(banks[j], codes["dom", j], E5M2, 0, pw_mx, E4M3, True, False)
-            product(banks[j], codes["qm", j], E4M3, 0, ds_mx, E5M2, False, True)
-            results[j] = sbuf("result%d" % j, [P, N], F32)
+            for name in (first, second):
+                product(banks[j], codes[name, j], moving[name][0], 0, moving[name][1], moving[name][2],
+                        name == first, name == second)
 
-        def empty(j, lo, hi):
-            nc.scalar.copy(out=results[j][:, lo:hi], in_=banks[j][:, lo:hi])
+        def empty(j, lo, hi, tag):
+            results[j, lo] = sbuf(tag, [P, hi - lo], F32)
+            nc.scalar.copy(out=results[j, lo][:], in_=banks[j][:, lo:hi])
 
         def scatter(j, lo, hi):
-            nc.vector.tensor_copy(windows[j][:].indirect(offsets[:, lo // BAND : hi // BAND]), results[j][:, lo:hi])
+            nc.vector.tensor_copy(windows[j][:].indirect(offsets[:, lo // BAND : hi // BAND]), results[j, lo][:])
 
         def store(j):
             nc.sync.dma_start(out=out[j * P : (j + 1) * P, :], in_=windows[j][:])
 
-        flip_qm([0], "flipped0")
+        flip_qm(0, 0, sbuf("flipped0", [P, PACK, P], BF16)[:])
+        weave_slots(nc.scalar.copy, pw_woven, pw, PW_SPLIT, N)
         weave_block("dom", 0, nc.scalar.copy, "dom_woven0")
-        weave_slots(nc.scalar.copy, pw_woven, pw, N // 2, N)
-        weave_block("qm", 0, nc.scalar.copy, "qm_woven0")
         weave_slots(nc.scalar.copy, ds_woven, ds, DS_SPLIT, N)
-        quantize(pw_mx, pw_woven, E4M3, 0, N // 2)
-        weave_slots(nc.vector.tensor_copy, ds_woven, ds, 0, DS_SPLIT)
+        weave_block("qm", 0, nc.scalar.copy, "qm_woven0")
+        quantize(pw_mx, pw_woven, E4M3, 0, N)
         quantize_block("dom", 0)
-        quantize(pw_mx, pw_woven, E4M3, N // 2, N)
+        weave_slots(nc.vector.tensor_copy, ds_woven, ds, 0, DS_SPLIT)
+        quantize(ds_mx, ds_woven, E5M2, N // 2, N)
         quantize(ds_mx, ds_woven, E5M2, 0, N // 2)
         quantize_block("qm", 0)
-        quantize(ds_mx, ds_woven, E5M2, N // 2, N)
-        products(0)
+        products(0, "dom", "qm")
 
-        pair = sbuf("ds", [P, 2, P * PACK], BF16)
-        for u in range(2):
-            woven["dom", 1 + u] = pair[:, u, :]
-            weave(nc.scalar.copy, pair[:, u, :], rows["dom", 1 + u])
-        flip_qm([1, 2], "ds_woven")
-        weave_block("qm", 1, nc.vector.tensor_copy, "pw_woven")
+        weave_block("dom", 1, nc.scalar.copy, "ds")
+        flipped = sbuf("ds_woven", [P, PACK, D - P], BF16)
+        flip_qm(1, 1, flipped[:, :, :P])
+        weave_block("qm", 1, nc.scalar.copy, "qm_woven1")
         quantize_block("dom", 1)
-        quantize_block("dom", 2)
+        flip_qm(2, 3, flipped[:, :, P:])
         quantize_block("qm", 1)
-        products(1)
+        products(1, "dom", "qm")
         for lo, hi in halves:
-            empty(0, lo, hi)
-        weave_block("qm", 2, nc.scalar.copy, "ds")
+            empty(0, lo, hi, "half%d" % lo)
         for lo, hi in halves:
             scatter(0, lo, hi)
         store(0)
-        quantize_block("qm", 2)
-        products(2)
-        flip_qm([3], "result0")
-        empty(1, 0, N)
-        weave_block("dom", 3, nc.scalar.copy, "ds_woven")
-        weave_block("qm", 3, nc.scalar.copy, "ds")
-        scatter(1, 0, N)
-        store(1)
-        quantize_block("dom", 3)
-        quantize_block("qm", 3)
-        products(3)
         for j in (2, 3):
-            empty(j, 0, N)
-            scatter(j, 0, N)
-            store(j)
+            weave_block("qm", j, nc.scalar.copy, "half0")
+            weave_block("dom", j, nc.vector.tensor_copy if j == 2 else nc.scalar.copy, "half%d" % (N // 2))
+            quantize_block("qm", j)
+            quantize_block("dom", j)
+            products(j, "qm", "dom")
+            empty(j - 1, 0, N, "result1" if j == 2 else "half%d" % (N // 2))
+            scatter(j - 1, 0, N)
+            store(j - 1)
+        empty(3, 0, N, "result3")
+        scatter(3, 0, N)
+        store(3)

@@ -73,7 +73,7 @@ def tile_attend_gat_tnh_c_kernel(tc, qT, cT, doT, rw, qm, dom, offs, out):
 
         q_raw = load("qT_raw", qT, 0, PACK)
         do_raw = load("doT_raw", doT, 0, PACK)
-        raw = {"dom": load("dom_raw", dom, 0, PACK), "qm": load("qm_raw", qm, 0, PACK)}
+        raw = {"qm": load("qm_raw", qm, 0, PACK), "dom": load("dom_raw", dom, 0, PACK)}
 
         windows = [sbuf("window%d" % j, [P, T], F32) for j in range(D // P)]
         for j in range(D // P - 1):
@@ -135,22 +135,6 @@ def tile_attend_gat_tnh_c_kernel(tc, qT, cT, doT, rw, qm, dom, offs, out):
         def slope(t):
             nc.vector.scalar_tensor_tensor(ds[:, t, :], sq[t][:], level[:, t : t + 1], dp[t][:], ALU.subtract, ALU.mult)
 
-        doT_mx = operand("doT", R)
-        dp = []
-        gated(0)
-        for t in range(PACK):
-            quantize(doT_mx, do_dealt, E5M2, t * P, (t + 1) * P)
-            bank = psum.tile([P, N], F32, name="second%d" % t)
-            product(bank, doT_mx, E5M2, t * P, c_mx, E4M3, True, True)
-            dp.append(bank)
-        for t in range(1, PACK):
-            gated(t)
-        nc.gpsimd.tensor_scalar(pw_woven[:, : PACK * PW_SPLIT].rearrange("p (n t) -> p n t", t=PACK),
-                                pw[:, :, :PW_SPLIT].rearrange("p t n -> p n t"), 1.0, 0.0, ALU.mult, ALU.add)
-        for t in range(PACK):
-            slope(t)
-
-        ds_woven = sbuf("ds_woven", [P, N * PACK], BF16)
         pw_mx = operand("pw", N)
         ds_mx = operand("ds", N)
         rows = {}
@@ -195,17 +179,36 @@ def tile_attend_gat_tnh_c_kernel(tc, qT, cT, doT, rw, qm, dom, offs, out):
         def store(j):
             nc.sync.dma_start(out=out[j * P : (j + 1) * P, :], in_=windows[j][:])
 
+        doT_mx = operand("doT", R)
+        dp = []
+        gated(0)
+        for t in range(PACK):
+            quantize(doT_mx, do_dealt, E5M2, t * P, (t + 1) * P)
+            bank = psum.tile([P, N], F32, name="second%d" % t)
+            product(bank, doT_mx, E5M2, t * P, c_mx, E4M3, True, True)
+            dp.append(bank)
+        for t in range(1, PACK - 1):
+            gated(t)
         flip_qm(0, 0, sbuf("flipped0", [P, PACK, P], BF16)[:])
+        gated(PACK - 1)
+        nc.gpsimd.tensor_scalar(pw_woven[:, : PACK * PW_SPLIT].rearrange("p (n t) -> p n t", t=PACK),
+                                pw[:, :, :PW_SPLIT].rearrange("p t n -> p n t"), 1.0, 0.0, ALU.mult, ALU.add)
+        for t in range(PACK):
+            slope(t)
+
+        ds_woven = sbuf("ds_woven", [P, N * PACK], BF16)
+        weave_block("qm", 0, nc.scalar.copy, "qm_woven0")
         weave_slots(nc.scalar.copy, pw_woven, pw, PW_SPLIT, N)
         weave_block("dom", 0, nc.scalar.copy, "dom_woven0")
-        weave_slots(nc.scalar.copy, ds_woven, ds, DS_SPLIT, N)
-        weave_block("qm", 0, nc.scalar.copy, "qm_woven0")
+        weave_slots(nc.scalar.copy, ds_woven, ds, DS_SPLIT, N - P)
+        weave_slots(nc.scalar.copy, ds_woven, ds, N - P, N)
         quantize(pw_mx, pw_woven, E4M3, 0, N)
-        quantize_block("dom", 0)
         weave_slots(nc.vector.tensor_copy, ds_woven, ds, 0, DS_SPLIT)
-        quantize(ds_mx, ds_woven, E5M2, N // 2, N)
-        quantize(ds_mx, ds_woven, E5M2, 0, N // 2)
+        quantize_block("dom", 0)
         quantize_block("qm", 0)
+        quantize(ds_mx, ds_woven, E5M2, 0, P)
+        quantize(ds_mx, ds_woven, E5M2, P, N - P)
+        quantize(ds_mx, ds_woven, E5M2, N - P, N)
         products(0, "dom", "qm")
 
         weave_block("dom", 1, nc.scalar.copy, "ds")

@@ -155,6 +155,18 @@ def tile_attend_gat_tnh_c_kernel(tc, qT, cT, doT, rw, qm, dom, offs, out):
             woven[name, j] = sbuf(tag, [P, P * PACK], BF16)[:]
             weave(copy, woven[name, j], rows[name, j])
 
+        def flip_on_scalar(j, flipped):
+            for t in range(PACK):
+                nc.scalar.activation(out=flipped[:, t, :], in_=raw["qm"][:, t, j * P : (j + 1) * P], func=ACT.Copy,
+                                     scale=flip[:, t : t + 1])
+            rows["qm", j] = flipped
+
+        def flip_and_weave(j, tag):
+            woven["qm", j] = sbuf(tag, [P, P * PACK], BF16)[:]
+            nc.vector.tensor_tensor(woven["qm", j].rearrange("p (c i t) -> p c t i", i=RUN, t=PACK),
+                                    raw["qm"][:, :, j * P : (j + 1) * P].rearrange("p t (c i) -> p c t i", i=RUN),
+                                    flip[:].unsqueeze(1).unsqueeze(3).to_broadcast([P, P // RUN, PACK, RUN]), ALU.mult)
+
         def quantize_block(name, j):
             codes[name, j] = operand("%s%d" % (name, j), P)
             quantize(codes[name, j], woven[name, j], E4M3 if name == "qm" else E5M2, 0, P)
@@ -211,28 +223,34 @@ def tile_attend_gat_tnh_c_kernel(tc, qT, cT, doT, rw, qm, dom, offs, out):
         quantize(ds_mx, ds_woven, E5M2, N - P, N)
         products(0, "dom", "qm")
 
-        weave_block("dom", 1, nc.scalar.copy, "ds")
-        flipped = sbuf("ds_woven", [P, PACK, D - P], BF16)
-        flip_qm(1, 1, flipped[:, :, :P])
-        weave_block("qm", 1, nc.scalar.copy, "qm_woven1")
+        pair = sbuf("ds", [P, 2, P * PACK], BF16)
+        woven["dom", 1] = pair[:, 0, :]
+        weave(nc.scalar.copy, woven["dom", 1], rows["dom", 1])
+        flip_on_scalar(2, pair[:, 1, :].rearrange("p (t c) -> p t c", t=PACK))
+        flip_and_weave(1, "ds_woven")
         quantize_block("dom", 1)
-        flip_qm(2, 3, flipped[:, :, P:])
         quantize_block("qm", 1)
         products(1, "dom", "qm")
         for lo, hi in halves:
             empty(0, lo, hi, "half%d" % lo)
+        weave_block("qm", 2, nc.scalar.copy, "qm_woven2")
         for lo, hi in halves:
             scatter(0, lo, hi)
         store(0)
+        weave_block("dom", 2, nc.vector.tensor_copy, "ds_woven")
+        quantize_block("qm", 2)
+        quantize_block("dom", 2)
+        products(2, "qm", "dom")
+        empty(1, 0, N, "result1")
+        flip_on_scalar(3, sbuf("half0", [P, PACK, P], BF16)[:])
+        weave_block("qm", 3, nc.scalar.copy, "qm_woven3")
+        scatter(1, 0, N)
+        store(1)
+        weave_block("dom", 3, nc.vector.tensor_copy, "result1")
+        quantize_block("qm", 3)
+        quantize_block("dom", 3)
+        products(3, "qm", "dom")
         for j in (2, 3):
-            weave_block("qm", j, nc.scalar.copy, "half0")
-            weave_block("dom", j, nc.vector.tensor_copy if j == 2 else nc.scalar.copy, "half%d" % (N // 2))
-            quantize_block("qm", j)
-            quantize_block("dom", j)
-            products(j, "qm", "dom")
-            empty(j - 1, 0, N, "result1" if j == 2 else "half%d" % (N // 2))
-            scatter(j - 1, 0, N)
-            store(j - 1)
-        empty(3, 0, N, "result3")
-        scatter(3, 0, N)
-        store(3)
+            empty(j, 0, N, "qm_woven3" if j == 2 else "result3")
+            scatter(j, 0, N)
+            store(j)

@@ -8,6 +8,7 @@ FLOPS = 4 * 2 * D * R * N
 F32 = mybir.dt.float32
 BF16 = mybir.dt.bfloat16
 U32 = mybir.dt.uint32
+I32 = mybir.dt.int32
 U16 = mybir.dt.uint16
 U8 = mybir.dt.uint8
 E4M3 = mybir.dt.float8_e4m3fn_x4
@@ -21,6 +22,7 @@ BAND = 16
 RUN = 4
 DS_SPLIT = 192
 PW_SPLIT = 384
+FLIP_SPLIT = 3
 
 
 def tile_attend_gat_tnh_c_kernel(tc, qT, cT, doT, rw, qm, dom, offs, out):
@@ -92,16 +94,17 @@ def tile_attend_gat_tnh_c_kernel(tc, qT, cT, doT, rw, qm, dom, offs, out):
         flip = sbuf("flip", [P, PACK], F32)
         nc.gpsimd.tensor_scalar(flip[:], below[:], 1.0, -1.0, ALU.mult, ALU.add)
 
-        c_woven = sbuf("c_woven", [P, N * PACK], BF16)
-        c_places = c_woven[:].rearrange("p (n t) -> p t n", t=PACK)
-        for t in range(PACK - 1):
-            nc.vector.tensor_copy(c_places[:, t, :], planes[t][:].indirect(offsets[:]))
-        for lo, hi in halves:
-            nc.vector.tensor_copy(c_places[:, PACK - 1, lo:hi],
-                                  planes[PACK - 1][:].indirect(offsets[:, lo // BAND : hi // BAND]))
+        c_pairs = [sbuf("c_pairs%d" % h, [P, 2, N // 2, 2], BF16) for h in range(2)]
+        for t in range(PACK):
+            for h, (lo, hi) in enumerate(halves):
+                nc.vector.tensor_copy(c_pairs[h][:, t // 2, :, t % 2], planes[t][:].indirect(offsets[:, lo // BAND : hi // BAND]))
+        c_woven = [sbuf("c_woven%d" % h, [P, N // 2 * PACK], BF16) for h in range(2)]
+        for h in range(2):
+            nc.vector.tensor_copy(out=c_woven[h][:].bitcast(I32).rearrange("p (c i u) -> p c u i", i=RUN, u=2),
+                                  in_=c_pairs[h][:].rearrange("p u n e -> p u (n e)").bitcast(I32).rearrange("p u (c i) -> p c u i", i=RUN))
         c_mx = operand("c", N)
-        for lo, hi in halves:
-            quantize(c_mx, c_woven, E4M3, lo, hi)
+        for h, (lo, hi) in enumerate(halves):
+            nc.vector.quantize_mx(out=c_mx[0][:, lo:hi].bitcast(E4M3), scales=c_mx[1][:, lo:hi], in_=c_woven[h][:])
 
         q_dealt = sbuf("q_dealt", [P, R * PACK], BF16)
         deal(nc.vector.tensor_copy, q_dealt, q_raw[:], (0, PACK), (0, 2))
@@ -141,12 +144,9 @@ def tile_attend_gat_tnh_c_kernel(tc, qT, cT, doT, rw, qm, dom, offs, out):
         woven = {}
         codes = {}
 
-        def flip_qm(first, last, flipped):
-            for t in range(PACK):
-                nc.vector.tensor_scalar(flipped[:, t, :], raw["qm"][:, t, first * P : (last + 1) * P],
-                                        flip[:, t : t + 1], None, ALU.mult)
-            for j in range(first, last + 1):
-                rows["qm", j] = flipped[:, :, (j - first) * P : (j - first + 1) * P]
+        def flip_on_vector(j, flipped, places):
+            for t in places:
+                nc.vector.tensor_scalar(flipped[:, t, :], raw["qm"][:, t, j * P : (j + 1) * P], flip[:, t : t + 1], None, ALU.mult)
 
         for j in range(D // P):
             rows["dom", j] = raw["dom"][:, :, j * P : (j + 1) * P]
@@ -155,8 +155,8 @@ def tile_attend_gat_tnh_c_kernel(tc, qT, cT, doT, rw, qm, dom, offs, out):
             woven[name, j] = sbuf(tag, [P, P * PACK], BF16)[:]
             weave(copy, woven[name, j], rows[name, j])
 
-        def flip_on_scalar(j, flipped):
-            for t in range(PACK):
+        def flip_on_scalar(j, flipped, places=range(PACK)):
+            for t in places:
                 nc.scalar.activation(out=flipped[:, t, :], in_=raw["qm"][:, t, j * P : (j + 1) * P], func=ACT.Copy,
                                      scale=flip[:, t : t + 1])
             rows["qm", j] = flipped
@@ -201,7 +201,8 @@ def tile_attend_gat_tnh_c_kernel(tc, qT, cT, doT, rw, qm, dom, offs, out):
             dp.append(bank)
         for t in range(1, PACK - 1):
             gated(t)
-        flip_qm(0, 0, sbuf("flipped0", [P, PACK, P], BF16)[:])
+        flipped0 = sbuf("flipped0", [P, PACK, P], BF16)
+        flip_on_vector(0, flipped0[:], range(FLIP_SPLIT))
         gated(PACK - 1)
         nc.gpsimd.tensor_scalar(pw_woven[:, : PACK * PW_SPLIT].rearrange("p (n t) -> p n t", t=PACK),
                                 pw[:, :, :PW_SPLIT].rearrange("p t n -> p n t"), 1.0, 0.0, ALU.mult, ALU.add)
@@ -209,8 +210,9 @@ def tile_attend_gat_tnh_c_kernel(tc, qT, cT, doT, rw, qm, dom, offs, out):
             slope(t)
 
         ds_woven = sbuf("ds_woven", [P, N * PACK], BF16)
-        weave_block("qm", 0, nc.scalar.copy, "qm_woven0")
+        flip_on_scalar(0, flipped0[:], range(FLIP_SPLIT, PACK))
         weave_slots(nc.scalar.copy, pw_woven, pw, PW_SPLIT, N)
+        weave_block("qm", 0, nc.scalar.copy, "qm_woven0")
         weave_block("dom", 0, nc.scalar.copy, "dom_woven0")
         weave_slots(nc.scalar.copy, ds_woven, ds, DS_SPLIT, N - P)
         weave_slots(nc.scalar.copy, ds_woven, ds, N - P, N)

@@ -57,6 +57,7 @@ def tile_attend_gat_tnh_c_kernel(tc, qT, cT, doT, rw, qm, dom, offs, out):
                  in_=src.rearrange("p j (s t) -> p s j t", t=PACK)[:, :, :, places[0] : places[1]])
 
         halves = [(0, N // 2), (N // 2, N)]
+        pieces = [(0, P), (P, N)]
 
         offsets = sbuf("offsets", [P, N // BAND], U16)
         planes = [sbuf("plane%d" % t, [P, T], F32) for t in range(PACK)]
@@ -83,6 +84,8 @@ def tile_attend_gat_tnh_c_kernel(tc, qT, cT, doT, rw, qm, dom, offs, out):
         nc.gpsimd.memset(windows[D // P - 1][:], 0.0)
         size = sbuf("size", [P, PACK], F32)
         nc.scalar.activation(out=size[:], in_=gate[:], func=ACT.Abs)
+        zeros = sbuf("zeros", [P, P], F32)
+        nc.gpsimd.memset(zeros[:], 0.0)
         half = sbuf("half", [P, PACK], F32)
         nc.gpsimd.memset(half[:], 0.5)
         root = sbuf("root", [P, PACK], F32)
@@ -233,26 +236,25 @@ def tile_attend_gat_tnh_c_kernel(tc, qT, cT, doT, rw, qm, dom, offs, out):
         quantize_block("dom", 1)
         quantize_block("qm", 1)
         products(1, "dom", "qm")
-        for lo, hi in halves:
+        for lo, hi in pieces:
             empty(0, lo, hi, "half%d" % lo)
         weave_block("qm", 2, nc.scalar.copy, "qm_woven2")
-        for lo, hi in halves:
-            scatter(0, lo, hi)
+        nc.vector.tensor_tensor(windows[0][:].indirect(offsets[:, : P // BAND]), results[0, 0][:], zeros[:], ALU.add)
+        scatter(0, P, N)
         store(0)
         weave_block("dom", 2, nc.vector.tensor_copy, "ds_woven")
         quantize_block("qm", 2)
         quantize_block("dom", 2)
         products(2, "qm", "dom")
         empty(1, 0, N, "result1")
-        flip_on_scalar(3, sbuf("half0", [P, PACK, P], BF16)[:])
-        weave_block("qm", 3, nc.scalar.copy, "qm_woven3")
+        weave_block("dom", 3, nc.scalar.copy, "half0")
         scatter(1, 0, N)
         store(1)
-        weave_block("dom", 3, nc.vector.tensor_copy, "result1")
-        quantize_block("qm", 3)
+        flip_and_weave(3, "qm_woven2")
         quantize_block("dom", 3)
-        products(3, "qm", "dom")
+        quantize_block("qm", 3)
+        products(3, "dom", "qm")
         for j in (2, 3):
-            empty(j, 0, N, "qm_woven3" if j == 2 else "result3")
+            empty(j, 0, N, "result%d" % j)
             scatter(j, 0, N)
             store(j)

@@ -164,12 +164,6 @@ def tile_attend_gat_tnh_c_kernel(tc, qT, cT, doT, rw, qm, dom, offs, out):
                                      scale=flip[:, t : t + 1])
             rows["qm", j] = flipped
 
-        def flip_and_weave(j, tag):
-            woven["qm", j] = sbuf(tag, [P, P * PACK], BF16)[:]
-            nc.vector.tensor_tensor(woven["qm", j].rearrange("p (c i t) -> p c t i", i=RUN, t=PACK),
-                                    raw["qm"][:, :, j * P : (j + 1) * P].rearrange("p t (c i) -> p c t i", i=RUN),
-                                    flip[:].unsqueeze(1).unsqueeze(3).to_broadcast([P, P // RUN, PACK, RUN]), ALU.mult)
-
         def quantize_block(name, j):
             codes[name, j] = operand("%s%d" % (name, j), P)
             quantize(codes[name, j], woven[name, j], E4M3 if name == "qm" else E5M2, 0, P)
@@ -232,14 +226,17 @@ def tile_attend_gat_tnh_c_kernel(tc, qT, cT, doT, rw, qm, dom, offs, out):
         woven["dom", 1] = pair[:, 0, :]
         weave(nc.scalar.copy, woven["dom", 1], rows["dom", 1])
         flip_on_scalar(2, pair[:, 1, :].rearrange("p (t c) -> p t c", t=PACK))
-        flip_and_weave(1, "ds_woven")
+        flipped1 = sbuf("ds_woven", [P, PACK, P], BF16)
+        flip_on_vector(1, flipped1[:], range(PACK))
+        rows["qm", 1] = flipped1[:]
         quantize_block("dom", 1)
-        quantize_block("qm", 1)
-        products(1, "dom", "qm")
+        weave_block("qm", 1, nc.vector.tensor_copy, "pw_woven")
         for lo, hi in pieces:
             empty(0, lo, hi, "half%d" % lo)
         weave_block("qm", 2, nc.scalar.copy, "qm_woven2")
         nc.vector.tensor_tensor(windows[0][:].indirect(offsets[:, : P // BAND]), results[0, 0][:], zeros[:], ALU.add)
+        quantize_block("qm", 1)
+        products(1, "dom", "qm")
         scatter(0, P, N)
         store(0)
         weave_block("dom", 2, nc.vector.tensor_copy, "ds_woven")
@@ -247,10 +244,11 @@ def tile_attend_gat_tnh_c_kernel(tc, qT, cT, doT, rw, qm, dom, offs, out):
         quantize_block("dom", 2)
         products(2, "qm", "dom")
         empty(1, 0, N, "result1")
-        weave_block("dom", 3, nc.scalar.copy, "half0")
+        flip_on_scalar(3, sbuf("half0", [P, PACK, P], BF16)[:])
+        weave_block("dom", 3, nc.scalar.copy, "half%d" % P)
         scatter(1, 0, N)
         store(1)
-        flip_and_weave(3, "qm_woven2")
+        weave_block("qm", 3, nc.vector.tensor_copy, "qm_woven2")
         quantize_block("dom", 3)
         quantize_block("qm", 3)
         products(3, "dom", "qm")

@@ -129,8 +129,12 @@ def tile_attend_gat_tnh_c_kernel(tc, qT, cT, doT, rw, qm, dom, offs, out):
         sq = [sbuf("sq%d" % t, [P, N], F32) for t in range(PACK)]
         for t in range(PACK):
             nc.scalar.activation(out=p[t][:], in_=scores[t][:], func=ACT.Tanh)
-        for t in range(PACK):
+
+        def square(t):
             nc.scalar.activation(out=sq[t][:], in_=p[t][:], func=ACT.Square, scale=root[:, t : t + 1])
+
+        for t in range(PACK - 1):
+            square(t)
 
         def weave_slots(copy, dst, src, lo, hi):
             weave(copy, dst[:, PACK * lo : PACK * hi], src[:, :, lo:hi])
@@ -200,6 +204,8 @@ def tile_attend_gat_tnh_c_kernel(tc, qT, cT, doT, rw, qm, dom, offs, out):
             gated(t)
         flipped0 = sbuf("flipped0", [P, PACK, P], BF16)
         flip_on_vector(0, flipped0[:], range(FLIP_SPLIT))
+        flip_on_scalar(0, flipped0[:], range(FLIP_SPLIT, PACK))
+        square(PACK - 1)
         gated(PACK - 1)
         nc.gpsimd.tensor_scalar(pw_woven[:, : PACK * PW_SPLIT].rearrange("p (n t) -> p n t", t=PACK),
                                 pw[:, :, :PW_SPLIT].rearrange("p t n -> p n t"), 1.0, 0.0, ALU.mult, ALU.add)
@@ -207,16 +213,15 @@ def tile_attend_gat_tnh_c_kernel(tc, qT, cT, doT, rw, qm, dom, offs, out):
             slope(t)
 
         ds_woven = sbuf("ds_woven", [P, N * PACK], BF16)
-        flip_on_scalar(0, flipped0[:], range(FLIP_SPLIT, PACK))
-        weave_slots(nc.scalar.copy, pw_woven, pw, PW_SPLIT, N)
         weave_block("qm", 0, nc.scalar.copy, "qm_woven0")
+        weave_slots(nc.scalar.copy, pw_woven, pw, PW_SPLIT, N)
         weave_block("dom", 0, nc.scalar.copy, "dom_woven0")
         weave_slots(nc.scalar.copy, ds_woven, ds, DS_SPLIT, N - P)
         weave_slots(nc.scalar.copy, ds_woven, ds, N - P, N)
+        quantize_block("qm", 0)
         quantize(pw_mx, pw_woven, E4M3, 0, N)
         weave_slots(nc.vector.tensor_copy, ds_woven, ds, 0, DS_SPLIT)
         quantize_block("dom", 0)
-        quantize_block("qm", 0)
         quantize(ds_mx, ds_woven, E5M2, 0, P)
         quantize(ds_mx, ds_woven, E5M2, P, N - P)
         quantize(ds_mx, ds_woven, E5M2, N - P, N)

@@ -1,6 +1,7 @@
 from contextlib import ExitStack
 
 import concourse.mybir as mybir
+from concourse.masks import make_identity
 
 N, T, D, R = 512, 2048, 512, 512
 FLOPS = 4 * 2 * D * R * N
@@ -60,14 +61,24 @@ def tile_attend_gat_tnh_c_kernel(tc, qT, cT, doT, rw, qm, dom, offs, out):
         pieces = [(0, P), (P, N)]
 
         offsets = sbuf("offsets", [P, N // BAND], U16)
-        planes = [sbuf("plane%d" % t, [P, T], F32) for t in range(PACK)]
-        c_rows = cT.rearrange("(p t) n -> t p n", t=PACK)
-        nc.sync.dma_start(out=planes[0][:], in_=c_rows[0])
+        c_rows = cT.rearrange("(p t) n -> p t n", t=PACK)
+        first_two = sbuf("planes01", [P, 2, T], F32)
+        nc.sync.dma_start(out=first_two[:], in_=c_rows[:, :2, :])
+        gate_row = sbuf("gate_row", [P, R], F32)
+        nc.gpsimd.memset(gate_row[:], 0.0)
+        nc.sync.dma_start(out=gate_row[:1, :], in_=rw[0].rearrange("r o -> o r"))
         nc.sync.dma_start(offsets[:], offs)
-        for t in range(1, PACK):
-            nc.sync.dma_start(out=planes[t][:], in_=c_rows[t])
+        planes = [first_two[:, 0, :], first_two[:, 1, :]]
+        for t in range(2, PACK):
+            planes.append(sbuf("plane%d" % t, [P, T], F32)[:])
+            nc.sync.dma_start(out=planes[t], in_=c_rows[:, t, :])
+        ident = sbuf("ident", [P, P], F32)
+        make_identity(nc, ident[:])
+        turned = psum.tile([P, PACK, P], F32, name="first0")
+        for t in range(PACK):
+            nc.tensor.transpose(turned[:, t, :], gate_row[:, t::PACK], ident[:])
         gate = sbuf("gate", [P, PACK], F32)
-        nc.scalar.dma_start(out=gate[:], in_=rw[0].rearrange("(p t) o -> p (t o)", t=PACK))
+        nc.scalar.copy(out=gate[:], in_=turned[:, :, 0])
 
         def load(name, src, lo, hi):
             tile = sbuf(name, [P, hi - lo, src.shape[2]], F32)
@@ -100,7 +111,7 @@ def tile_attend_gat_tnh_c_kernel(tc, qT, cT, doT, rw, qm, dom, offs, out):
         c_pairs = [sbuf("c_pairs%d" % h, [P, 2, N // 2, 2], BF16) for h in range(2)]
         for t in range(PACK):
             for h, (lo, hi) in enumerate(halves):
-                nc.vector.tensor_copy(c_pairs[h][:, t // 2, :, t % 2], planes[t][:].indirect(offsets[:, lo // BAND : hi // BAND]))
+                nc.vector.tensor_copy(c_pairs[h][:, t // 2, :, t % 2], planes[t].indirect(offsets[:, lo // BAND : hi // BAND]))
         c_woven = [sbuf("c_woven%d" % h, [P, N // 2 * PACK], BF16) for h in range(2)]
         for h in range(2):
             nc.vector.tensor_copy(out=c_woven[h][:].bitcast(I32).rearrange("p (c i u) -> p c u i", i=RUN, u=2),

@@ -205,12 +205,16 @@ def tile_attend_gat_tnh_c_kernel(tc, qT, cT, doT, rw, qm, dom, offs, out):
 
         doT_mx = operand("doT", R)
         dp = []
+
+        def gradient(t):
+            dp.append(psum.tile([P, N], F32, name="second%d" % (t % (PACK - 1))))
+            product(dp[t], doT_mx, E5M2, t * P, c_mx, E4M3, True, True)
+
         gated(0)
         for t in range(PACK):
             quantize(doT_mx, do_dealt, E5M2, t * P, (t + 1) * P)
-            bank = psum.tile([P, N], F32, name="second%d" % t)
-            product(bank, doT_mx, E5M2, t * P, c_mx, E4M3, True, True)
-            dp.append(bank)
+            if t < PACK - 1:
+                gradient(t)
         for t in range(1, PACK - 1):
             gated(t)
         flipped0 = sbuf("flipped0", [P, PACK, P], BF16)
@@ -220,9 +224,12 @@ def tile_attend_gat_tnh_c_kernel(tc, qT, cT, doT, rw, qm, dom, offs, out):
         gated(PACK - 1)
         nc.gpsimd.tensor_scalar(pw_woven[:, : PACK * PW_SPLIT].rearrange("p (n t) -> p n t", t=PACK),
                                 pw[:, :, :PW_SPLIT].rearrange("p t n -> p n t"), 1.0, 0.0, ALU.mult, ALU.add)
-        for t in range(PACK):
+        slope(0)
+        gradient(PACK - 1)
+        for t in range(1, PACK):
             slope(t)
 
+        product(psum.tile([P, N], F32, name="second2"), qT_mx, E4M3, 0, c_mx, E4M3, True, True)
         ds_woven = sbuf("ds_woven", [P, N * PACK], BF16)
         weave_block("qm", 0, nc.scalar.copy, "qm_woven0")
         weave_slots(nc.scalar.copy, pw_woven, pw, PW_SPLIT, N)
@@ -230,11 +237,12 @@ def tile_attend_gat_tnh_c_kernel(tc, qT, cT, doT, rw, qm, dom, offs, out):
         weave_slots(nc.scalar.copy, ds_woven, ds, DS_SPLIT, N - P)
         weave_slots(nc.scalar.copy, ds_woven, ds, N - P, N)
         quantize_block("qm", 0)
+        product(psum.tile([P, N], F32, name="second1"), codes["qm", 0], E4M3, 0, c_mx, E4M3, True, True)
         quantize(pw_mx, pw_woven, E4M3, 0, N)
-        weave_slots(nc.vector.tensor_copy, ds_woven, ds, 0, DS_SPLIT)
         quantize_block("dom", 0)
-        quantize(ds_mx, ds_woven, E5M2, 0, P)
-        quantize(ds_mx, ds_woven, E5M2, P, N - P)
+        weave_slots(nc.vector.tensor_copy, ds_woven, ds, 0, DS_SPLIT)
+        quantize(ds_mx, ds_woven, E5M2, N // 2, N - P)
+        quantize(ds_mx, ds_woven, E5M2, 0, N // 2)
         quantize(ds_mx, ds_woven, E5M2, N - P, N)
         products(0, "dom", "qm")
 

@@ -246,37 +246,38 @@ def tile_attend_gat_tnh_c_kernel(tc, qT, cT, doT, rw, qm, dom, offs, out):
         quantize(ds_mx, ds_woven, E5M2, N - P, N)
         products(0, "dom", "qm")
 
-        pair = sbuf("ds", [P, 2, P * PACK], BF16)
-        woven["dom", 1] = pair[:, 0, :]
-        weave(nc.scalar.copy, woven["dom", 1], rows["dom", 1])
-        flip_on_scalar(2, pair[:, 1, :].rearrange("p (t c) -> p t c", t=PACK))
-        flipped1 = sbuf("ds_woven", [P, PACK, P], BF16)
-        flip_on_vector(1, flipped1[:], range(PACK))
-        rows["qm", 1] = flipped1[:]
+        weave_block("dom", 1, nc.scalar.copy, "ds")
+        flipped = sbuf("ds_woven", [P, PACK + 2, P], BF16)
+        flip_on_vector(1, flipped[:, 2:, :], range(PACK))
+        rows["qm", 1] = flipped[:, 2:, :]
+        flip_on_scalar(2, flipped[:, :PACK, :], range(2))
         quantize_block("dom", 1)
         weave_block("qm", 1, nc.vector.tensor_copy, "pw_woven")
         for lo, hi in pieces:
             empty(0, lo, hi, "half%d" % lo)
+        flip_on_scalar(2, flipped[:, :PACK, :], range(2, PACK))
         weave_block("qm", 2, nc.scalar.copy, "qm_woven2")
         nc.vector.tensor_tensor(windows[0][:].indirect(offsets[:, : P // BAND]), results[0, 0][:], zeros[:], ALU.add)
         quantize_block("qm", 1)
         products(1, "dom", "qm")
         scatter(0, P, N)
         store(0)
-        weave_block("dom", 2, nc.vector.tensor_copy, "ds_woven")
+        weave_block("dom", 2, nc.vector.tensor_copy, "half%d" % P)
         quantize_block("qm", 2)
         quantize_block("dom", 2)
         products(2, "qm", "dom")
-        empty(1, 0, N, "result1")
-        flip_on_scalar(3, sbuf("half0", [P, PACK, P], BF16)[:])
-        weave_block("dom", 3, nc.scalar.copy, "half%d" % P)
+        empty(1, 0, N, "ds_woven")
+        pair = sbuf("qm_woven2", [P, 2, P * PACK], BF16)
+        flip_on_scalar(3, pair[:, 0, :].rearrange("p (t c) -> p t c", t=PACK))
+        woven["dom", 3] = pair[:, 1, :]
+        weave(nc.scalar.copy, woven["dom", 3], rows["dom", 3])
         scatter(1, 0, N)
         store(1)
-        weave_block("qm", 3, nc.vector.tensor_copy, "qm_woven2")
+        weave_block("qm", 3, nc.vector.tensor_copy, "qm_woven3")
         quantize_block("dom", 3)
         quantize_block("qm", 3)
         products(3, "dom", "qm")
-        for j in (2, 3):
-            empty(j, 0, N, "result%d" % j)
+        for j, tag in ((2, "dom_raw"), (3, "result3")):
+            empty(j, 0, N, tag)
             scatter(j, 0, N)
             store(j)

@@ -262,7 +262,7 @@ def tile_attend_gat_tnh_c_kernel(tc, qT, cT, doT, rw, qm, dom, offs, out):
         products(1, "dom", "qm")
         scatter(0, P, N)
         store(0)
-        weave_block("dom", 2, nc.vector.tensor_copy, "half%d" % P)
+        weave_block("dom", 2, nc.vector.tensor_copy, "half0")
         quantize_block("qm", 2)
         quantize_block("dom", 2)
         products(2, "qm", "dom")

@@ -262,7 +262,9 @@ def tile_attend_gat_tnh_c_kernel(tc, qT, cT, doT, rw, qm, dom, offs, out):
         products(1, "dom", "qm")
         scatter(0, P, N)
         store(0)
-        weave_block("dom", 2, nc.vector.tensor_copy, "half0")
+        woven["dom", 2] = sbuf("pw_woven", [P, P * PACK], BF16)[:]
+        nc.gpsimd.tensor_scalar(woven["dom", 2].rearrange("p (n t) -> p n t", t=PACK),
+                                rows["dom", 2].rearrange("p t n -> p n t"), 1.0, 0.0, ALU.mult, ALU.add)
         quantize_block("qm", 2)
         quantize_block("dom", 2)
         products(2, "qm", "dom")

@@ -256,7 +256,6 @@ def tile_attend_gat_tnh_c_kernel(tc, qT, cT, doT, rw, qm, dom, offs, out):
         for lo, hi in pieces:
             empty(0, lo, hi, "half%d" % lo)
         flip_on_scalar(2, flipped[:, :PACK, :], range(2, PACK))
-        weave_block("qm", 2, nc.scalar.copy, "qm_woven2")
         nc.vector.tensor_tensor(windows[0][:].indirect(offsets[:, : P // BAND]), results[0, 0][:], zeros[:], ALU.add)
         quantize_block("qm", 1)
         products(1, "dom", "qm")
@@ -265,11 +264,12 @@ def tile_attend_gat_tnh_c_kernel(tc, qT, cT, doT, rw, qm, dom, offs, out):
         woven["dom", 2] = sbuf("pw_woven", [P, P * PACK], BF16)[:]
         nc.gpsimd.tensor_scalar(woven["dom", 2].rearrange("p (n t) -> p n t", t=PACK),
                                 rows["dom", 2].rearrange("p t n -> p n t"), 1.0, 0.0, ALU.mult, ALU.add)
-        quantize_block("qm", 2)
+        empty(1, 0, N, "result1")
+        weave_block("qm", 2, nc.vector.tensor_copy, "qm_woven2")
         quantize_block("dom", 2)
-        products(2, "qm", "dom")
-        empty(1, 0, N, "ds_woven")
-        pair = sbuf("qm_woven2", [P, 2, P * PACK], BF16)
+        quantize_block("qm", 2)
+        products(2, "dom", "qm")
+        pair = sbuf("ds_woven", [P, 2, P * PACK], BF16)
         flip_on_scalar(3, pair[:, 0, :].rearrange("p (t c) -> p t c", t=PACK))
         woven["dom", 3] = pair[:, 1, :]
         weave(nc.scalar.copy, woven["dom", 3], rows["dom", 3])

@@ -43,10 +43,10 @@ def tile_attend_gat_tnh_c_kernel(tc, qT, cT, doT, rw, qm, dom, offs, out):
             nc.vector.quantize_mx(out=codes[:, lo:hi].bitcast(fmt), scales=scales[:, lo:hi],
                                   in_=src[:, PACK * lo : PACK * hi])
 
-        def product(bank, stationary, stationary_fmt, lo, moving, moving_fmt, start, stop):
-            nc.tensor.matmul_mx(out=bank[:], lhsT=stationary[0][:, lo : lo + P].bitcast(stationary_fmt),
+        def product(bank, stationary, stationary_fmt, lo, moving, moving_fmt, start, stop, first=0, last=N):
+            nc.tensor.matmul_mx(out=bank, lhsT=stationary[0][:, lo : lo + P].bitcast(stationary_fmt),
                                 lhsT_scale=stationary[1][:, lo : lo + P],
-                                rhs=moving[0][:].bitcast(moving_fmt), rhs_scale=moving[1][:],
+                                rhs=moving[0][:, first:last].bitcast(moving_fmt), rhs_scale=moving[1][:, first:last],
                                 start=start, stop=stop)
 
         def weave(copy, dst, src):
@@ -58,7 +58,7 @@ def tile_attend_gat_tnh_c_kernel(tc, qT, cT, doT, rw, qm, dom, offs, out):
                  in_=src.rearrange("p j (s t) -> p s j t", t=PACK)[:, :, :, places[0] : places[1]])
 
         halves = [(0, N // 2), (N // 2, N)]
-        pieces = [(0, P), (P, N)]
+        half = N // 2
 
         offsets = sbuf("offsets", [P, N // BAND], U16)
         c_rows = cT.rearrange("(p t) n -> p t n", t=PACK)
@@ -95,12 +95,10 @@ def tile_attend_gat_tnh_c_kernel(tc, qT, cT, doT, rw, qm, dom, offs, out):
         nc.gpsimd.memset(windows[D // P - 1][:], 0.0)
         size = sbuf("size", [P, PACK], F32)
         nc.scalar.activation(out=size[:], in_=gate[:], func=ACT.Abs)
-        zeros = sbuf("zeros", [P, P], F32)
-        nc.gpsimd.memset(zeros[:], 0.0)
-        half = sbuf("half", [P, PACK], F32)
-        nc.gpsimd.memset(half[:], 0.5)
+        exponent = sbuf("exponent", [P, PACK], F32)
+        nc.gpsimd.memset(exponent[:], 0.5)
         root = sbuf("root", [P, PACK], F32)
-        nc.gpsimd.tensor_tensor(root[:], size[:], half[:], ALU.pow)
+        nc.gpsimd.tensor_tensor(root[:], size[:], exponent[:], ALU.pow)
         level = sbuf("level", [P, PACK], F32)
         nc.gpsimd.tensor_tensor(level[:], root[:], root[:], ALU.mult)
         below = sbuf("below", [P, PACK], F32)
@@ -128,7 +126,7 @@ def tile_attend_gat_tnh_c_kernel(tc, qT, cT, doT, rw, qm, dom, offs, out):
         for t in range(PACK):
             quantize(qT_mx, q_dealt, E4M3, t * P, (t + 1) * P)
             bank = psum.tile([P, N], F32, name="first%d" % t)
-            product(bank, qT_mx, E4M3, t * P, c_mx, E4M3, True, True)
+            product(bank[:], qT_mx, E4M3, t * P, c_mx, E4M3, True, True)
             scores.append(bank)
 
         do_dealt = sbuf("q_dealt", [P, R * PACK], BF16)
@@ -190,7 +188,7 @@ def tile_attend_gat_tnh_c_kernel(tc, qT, cT, doT, rw, qm, dom, offs, out):
             moving = {"dom": (E5M2, pw_mx, E4M3), "qm": (E4M3, ds_mx, E5M2)}
             banks[j] = psum.tile([P, N], F32, name="first%d" % j)
             for name in (first, second):
-                product(banks[j], codes[name, j], moving[name][0], 0, moving[name][1], moving[name][2],
+                product(banks[j][:], codes[name, j], moving[name][0], 0, moving[name][1], moving[name][2],
                         name == first, name == second)
 
         def empty(j, lo, hi, tag):
@@ -208,7 +206,7 @@ def tile_attend_gat_tnh_c_kernel(tc, qT, cT, doT, rw, qm, dom, offs, out):
 
         def gradient(t):
             dp.append(psum.tile([P, N], F32, name="second%d" % (t % (PACK - 1))))
-            product(dp[t], doT_mx, E5M2, t * P, c_mx, E4M3, True, True)
+            product(dp[t][:], doT_mx, E5M2, t * P, c_mx, E4M3, True, True)
 
         gated(0)
         for t in range(PACK):
@@ -229,7 +227,7 @@ def tile_attend_gat_tnh_c_kernel(tc, qT, cT, doT, rw, qm, dom, offs, out):
         for t in range(1, PACK):
             slope(t)
 
-        product(psum.tile([P, N], F32, name="second2"), qT_mx, E4M3, 0, c_mx, E4M3, True, True)
+        product(psum.tile([P, N], F32, name="second2")[:], qT_mx, E4M3, 0, c_mx, E4M3, True, True)
         ds_woven = sbuf("ds_woven", [P, N * PACK], BF16)
         weave_block("qm", 0, nc.scalar.copy, "qm_woven0")
         weave_slots(nc.scalar.copy, pw_woven, pw, PW_SPLIT, N)
@@ -237,45 +235,46 @@ def tile_attend_gat_tnh_c_kernel(tc, qT, cT, doT, rw, qm, dom, offs, out):
         weave_slots(nc.scalar.copy, ds_woven, ds, DS_SPLIT, N - P)
         weave_slots(nc.scalar.copy, ds_woven, ds, N - P, N)
         quantize_block("qm", 0)
-        product(psum.tile([P, N], F32, name="second1"), codes["qm", 0], E4M3, 0, c_mx, E4M3, True, True)
+        product(psum.tile([P, N], F32, name="second1")[:], codes["qm", 0], E4M3, 0, c_mx, E4M3, True, True)
+        weave_slots(nc.vector.tensor_copy, ds_woven, ds, 0, DS_SPLIT)
         quantize(pw_mx, pw_woven, E4M3, 0, N)
         quantize_block("dom", 0)
-        weave_slots(nc.vector.tensor_copy, ds_woven, ds, 0, DS_SPLIT)
-        quantize(ds_mx, ds_woven, E5M2, N // 2, N - P)
-        quantize(ds_mx, ds_woven, E5M2, 0, N // 2)
-        quantize(ds_mx, ds_woven, E5M2, N - P, N)
-        products(0, "dom", "qm")
+        first = [psum.tile([P, half], F32, name=name) for name in ("first0", "second0")]
+        for bank, (lo, hi) in zip(first, halves):
+            product(bank[:], codes["dom", 0], E5M2, 0, pw_mx, E4M3, True, False, lo, hi)
+        for bank, (lo, hi) in zip(first, halves):
+            quantize(ds_mx, ds_woven, E5M2, lo, hi)
+            product(bank[:], codes["qm", 0], E4M3, 0, ds_mx, E5M2, False, True, lo, hi)
 
-        weave_block("dom", 1, nc.scalar.copy, "ds")
-        flipped = sbuf("ds_woven", [P, PACK + 2, P], BF16)
-        flip_on_vector(1, flipped[:, 2:, :], range(PACK))
-        rows["qm", 1] = flipped[:, 2:, :]
-        flip_on_scalar(2, flipped[:, :PACK, :], range(2))
+        flip_on_scalar(1, sbuf("pw_woven", [P, PACK, P], BF16)[:])
+        weave_block("dom", 1, nc.vector.tensor_copy, "ds")
+        weave_block("qm", 1, nc.vector.tensor_copy, "qm_woven1")
+        low = sbuf("low", [P, half], F32)
+        high = sbuf("high", [P, half], F32)
+        nc.scalar.copy(out=low[:], in_=first[0][:])
+        nc.scalar.activation(windows[0][:].indirect(offsets[:, : half // BAND]), low[:], ACT.Copy)
+        nc.vector.tensor_copy(out=high[:], in_=first[1][:])
         quantize_block("dom", 1)
-        weave_block("qm", 1, nc.vector.tensor_copy, "pw_woven")
-        for lo, hi in pieces:
-            empty(0, lo, hi, "half%d" % lo)
-        flip_on_scalar(2, flipped[:, :PACK, :], range(2, PACK))
-        nc.vector.tensor_tensor(windows[0][:].indirect(offsets[:, : P // BAND]), results[0, 0][:], zeros[:], ALU.add)
         quantize_block("qm", 1)
         products(1, "dom", "qm")
-        scatter(0, P, N)
+        nc.vector.tensor_copy(windows[0][:].indirect(offsets[:, half // BAND :]), high[:])
         store(0)
-        woven["dom", 2] = sbuf("pw_woven", [P, P * PACK], BF16)[:]
+        flip_on_scalar(2, sbuf("low", [P, PACK, P], BF16)[:])
+        woven["dom", 2] = sbuf("qm_woven1", [P, P * PACK], BF16)[:]
         nc.gpsimd.tensor_scalar(woven["dom", 2].rearrange("p (n t) -> p n t", t=PACK),
                                 rows["dom", 2].rearrange("p t n -> p n t"), 1.0, 0.0, ALU.mult, ALU.add)
         empty(1, 0, N, "result1")
-        weave_block("qm", 2, nc.vector.tensor_copy, "qm_woven2")
+        weave_block("qm", 2, nc.vector.tensor_copy, "high")
         quantize_block("dom", 2)
+        scatter(1, 0, N)
+        store(1)
         quantize_block("qm", 2)
         products(2, "dom", "qm")
-        pair = sbuf("ds_woven", [P, 2, P * PACK], BF16)
+        pair = sbuf("low", [P, 2, P * PACK], BF16)
         flip_on_scalar(3, pair[:, 0, :].rearrange("p (t c) -> p t c", t=PACK))
         woven["dom", 3] = pair[:, 1, :]
         weave(nc.scalar.copy, woven["dom", 3], rows["dom", 3])
-        scatter(1, 0, N)
-        store(1)
-        weave_block("qm", 3, nc.vector.tensor_copy, "qm_woven3")
+        weave_block("qm", 3, nc.vector.tensor_copy, "result1")
         quantize_block("dom", 3)
         quantize_block("qm", 3)
         products(3, "dom", "qm")

@@ -237,12 +237,12 @@ def tile_attend_gat_tnh_c_kernel(tc, qT, cT, doT, rw, qm, dom, offs, out):
         quantize_block("qm", 0)
         product(psum.tile([P, N], F32, name="second1")[:], codes["qm", 0], E4M3, 0, c_mx, E4M3, True, True)
         weave_slots(nc.vector.tensor_copy, ds_woven, ds, 0, DS_SPLIT)
-        quantize(pw_mx, pw_woven, E4M3, 0, N)
-        quantize_block("dom", 0)
         first = [psum.tile([P, half], F32, name=name) for name in ("first0", "second0")]
         for bank, (lo, hi) in zip(first, halves):
+            quantize(pw_mx, pw_woven, E4M3, lo, hi)
+            if lo == 0:
+                quantize_block("dom", 0)
             product(bank[:], codes["dom", 0], E5M2, 0, pw_mx, E4M3, True, False, lo, hi)
-        for bank, (lo, hi) in zip(first, halves):
             quantize(ds_mx, ds_woven, E5M2, lo, hi)
             product(bank[:], codes["qm", 0], E4M3, 0, ds_mx, E5M2, False, True, lo, hi)
 

@@ -227,7 +227,7 @@ def tile_attend_gat_tnh_c_kernel(tc, qT, cT, doT, rw, qm, dom, offs, out):
         for t in range(1, PACK):
             slope(t)
 
-        product(psum.tile([P, N], F32, name="second2")[:], qT_mx, E4M3, 0, c_mx, E4M3, True, True)
+        product(psum.tile([P, half], F32, name="second2")[:], qT_mx, E4M3, 0, c_mx, E4M3, True, True, 0, half)
         ds_woven = sbuf("ds_woven", [P, N * PACK], BF16)
         weave_block("qm", 0, nc.scalar.copy, "qm_woven0")
         weave_slots(nc.scalar.copy, pw_woven, pw, PW_SPLIT, N)

@@ -199,7 +199,8 @@ def tile_attend_gat_tnh_c_kernel(tc, qT, cT, doT, rw, qm, dom, offs, out):
             nc.vector.tensor_copy(windows[j][:].indirect(offsets[:, lo // BAND : hi // BAND]), results[j, lo][:])
 
         def store(j):
-            nc.sync.dma_start(out=out[j * P : (j + 1) * P, :], in_=windows[j][:])
+            queue = nc.scalar if j % 2 else nc.sync
+            queue.dma_start(out=out[j * P : (j + 1) * P, :], in_=windows[j][:])
 
         doT_mx = operand("doT", R)
         dp = []

@@ -21,7 +21,7 @@ P = 128
 PACK = 4
 BAND = 16
 RUN = 4
-DS_SPLIT = 192
+DS_SPLIT = 224
 PW_SPLIT = 384
 FLIP_SPLIT = 3
 
@@ -233,8 +233,8 @@ def tile_attend_gat_tnh_c_kernel(tc, qT, cT, doT, rw, qm, dom, offs, out):
         weave_block("qm", 0, nc.scalar.copy, "qm_woven0")
         weave_slots(nc.scalar.copy, pw_woven, pw, PW_SPLIT, N)
         weave_block("dom", 0, nc.scalar.copy, "dom_woven0")
-        weave_slots(nc.scalar.copy, ds_woven, ds, DS_SPLIT, N - P)
-        weave_slots(nc.scalar.copy, ds_woven, ds, N - P, N)
+        weave_slots(nc.scalar.copy, ds_woven, ds, DS_SPLIT, half)
+        weave_slots(nc.scalar.copy, ds_woven, ds, half, N)
         quantize_block("qm", 0)
         product(psum.tile([P, N], F32, name="second1")[:], codes["qm", 0], E4M3, 0, c_mx, E4M3, True, True)
         weave_slots(nc.vector.tensor_copy, ds_woven, ds, 0, DS_SPLIT)

@@ -21,9 +21,10 @@ P = 128
 PACK = 4
 BAND = 16
 RUN = 4
-DS_SPLIT = 224
 PW_SPLIT = 384
-FLIP_SPLIT = 3
+FLIP_SPLIT = 2
+EARLY_SPLIT = 80
+LATE_SPLIT = 64
 
 
 def tile_attend_gat_tnh_c_kernel(tc, qT, cT, doT, rw, qm, dom, offs, out):
@@ -53,9 +54,9 @@ def tile_attend_gat_tnh_c_kernel(tc, qT, cT, doT, rw, qm, dom, offs, out):
             copy(out=dst.rearrange("p (c i t) -> p c t i", i=RUN, t=PACK),
                  in_=src.rearrange("p t (c i) -> p c t i", i=RUN))
 
-        def deal(copy, dst, src, rows, places):
-            copy(out=dst[:].rearrange("p (t s j) -> p s j t", t=PACK, j=PACK)[:, :, rows[0] : rows[1], places[0] : places[1]],
-                 in_=src.rearrange("p j (s t) -> p s j t", t=PACK)[:, :, :, places[0] : places[1]])
+        def deal(copy, dst, src, rows, places, cols=(0, P)):
+            copy(out=dst[:].rearrange("p (t s j) -> p s j t", t=PACK, j=PACK)[:, cols[0] : cols[1], rows[0] : rows[1], places[0] : places[1]],
+                 in_=src.rearrange("p j (s t) -> p s j t", t=PACK)[:, cols[0] : cols[1], :, places[0] : places[1]])
 
         halves = [(0, N // 2), (N // 2, N)]
         half = N // 2
@@ -86,8 +87,14 @@ def tile_attend_gat_tnh_c_kernel(tc, qT, cT, doT, rw, qm, dom, offs, out):
             return tile
 
         q_raw = load("qT_raw", qT, 0, PACK)
-        do_raw = load("doT_raw", doT, 0, PACK)
-        raw = {"qm": load("qm_raw", qm, 0, PACK), "dom": load("dom_raw", dom, 0, PACK)}
+        do_raw = [load("doT_raw%d" % h, doT, 2 * h, 2 * h + 2) for h in range(2)]
+        raw = {}
+        for lo, hi in ((0, P), (P, D)):
+            for name, src in (("qm", qm), ("dom", dom)):
+                tile = sbuf("%s_raw%d" % (name, lo), [P, PACK, hi - lo], F32)
+                nc.sync.dma_start(out=tile[:], in_=src[0].rearrange("(p j) w -> p j w", j=PACK)[:, :, lo:hi])
+                for j in range(lo // P, hi // P):
+                    raw[name, j] = tile[:, :, j * P - lo : (j + 1) * P - lo]
 
         windows = [sbuf("window%d" % j, [P, T], F32) for j in range(D // P)]
         for j in range(D // P - 1):
@@ -119,20 +126,25 @@ def tile_attend_gat_tnh_c_kernel(tc, qT, cT, doT, rw, qm, dom, offs, out):
             nc.vector.quantize_mx(out=c_mx[0][:, lo:hi].bitcast(E4M3), scales=c_mx[1][:, lo:hi], in_=c_woven[h][:])
 
         q_dealt = sbuf("q_dealt", [P, R * PACK], BF16)
-        deal(nc.vector.tensor_copy, q_dealt, q_raw[:], (0, PACK), (0, 2))
-        deal(nc.scalar.copy, q_dealt, q_raw[:], (0, PACK), (2, 4))
+        deal(nc.vector.tensor_copy, q_dealt, q_raw[:], (0, PACK), (0, 2), (0, EARLY_SPLIT))
+        deal(nc.scalar.copy, q_dealt, q_raw[:], (0, PACK), (0, 2), (EARLY_SPLIT, P))
+        deal(nc.vector.tensor_copy, q_dealt, q_raw[:], (0, PACK), (2, 4), (0, LATE_SPLIT // 2))
+        deal(nc.scalar.copy, q_dealt, q_raw[:], (0, PACK), (2, 4), (LATE_SPLIT, P))
         qT_mx = operand("qT", R)
         scores = []
         for t in range(PACK):
+            if t == 1:
+                deal(nc.vector.tensor_copy, q_dealt, q_raw[:], (0, PACK), (2, 4), (LATE_SPLIT // 2, LATE_SPLIT))
             quantize(qT_mx, q_dealt, E4M3, t * P, (t + 1) * P)
             bank = psum.tile([P, N], F32, name="first%d" % t)
             product(bank[:], qT_mx, E4M3, t * P, c_mx, E4M3, True, True)
             scores.append(bank)
 
         do_dealt = sbuf("q_dealt", [P, R * PACK], BF16)
-        deal(nc.vector.tensor_copy, do_dealt, do_raw[:], (0, PACK), (0, PACK))
+        for h in range(2):
+            deal(nc.vector.tensor_copy, do_dealt, do_raw[h][:], (2 * h, 2 * h + 2), (0, PACK))
         ds = sbuf("ds", [P, PACK, N], BF16)
-        pw = sbuf("doT_raw", [P, PACK, N], BF16)
+        pw = sbuf("doT_raw1", [P, PACK, N], BF16)
         pw_woven = sbuf("pw_woven", [P, N * PACK], BF16)
         p = [sbuf("p%d" % t, [P, N], F32) for t in range(PACK)]
         sq = [sbuf("sq%d" % t, [P, N], F32) for t in range(PACK)]
@@ -162,10 +174,10 @@ def tile_attend_gat_tnh_c_kernel(tc, qT, cT, doT, rw, qm, dom, offs, out):
 
         def flip_on_vector(j, flipped, places):
             for t in places:
-                nc.vector.tensor_scalar(flipped[:, t, :], raw["qm"][:, t, j * P : (j + 1) * P], flip[:, t : t + 1], None, ALU.mult)
+                nc.vector.tensor_scalar(flipped[:, t, :], raw["qm", j][:, t, :], flip[:, t : t + 1], None, ALU.mult)
 
         for j in range(D // P):
-            rows["dom", j] = raw["dom"][:, :, j * P : (j + 1) * P]
+            rows["dom", j] = raw["dom", j]
 
         def weave_block(name, j, copy, tag):
             woven[name, j] = sbuf(tag, [P, P * PACK], BF16)[:]
@@ -173,7 +185,7 @@ def tile_attend_gat_tnh_c_kernel(tc, qT, cT, doT, rw, qm, dom, offs, out):
 
         def flip_on_scalar(j, flipped, places=range(PACK)):
             for t in places:
-                nc.scalar.activation(out=flipped[:, t, :], in_=raw["qm"][:, t, j * P : (j + 1) * P], func=ACT.Copy,
+                nc.scalar.activation(out=flipped[:, t, :], in_=raw["qm", j][:, t, :], func=ACT.Copy,
                                      scale=flip[:, t : t + 1])
             rows["qm", j] = flipped
 
@@ -191,12 +203,12 @@ def tile_attend_gat_tnh_c_kernel(tc, qT, cT, doT, rw, qm, dom, offs, out):
                 product(banks[j][:], codes[name, j], moving[name][0], 0, moving[name][1], moving[name][2],
                         name == first, name == second)
 
-        def empty(j, lo, hi, tag):
-            results[j, lo] = sbuf(tag, [P, hi - lo], F32)
-            nc.scalar.copy(out=results[j, lo][:], in_=banks[j][:, lo:hi])
+        def empty(j, result):
+            results[j] = result
+            nc.scalar.copy(out=result, in_=banks[j][:])
 
-        def scatter(j, lo, hi):
-            nc.vector.tensor_copy(windows[j][:].indirect(offsets[:, lo // BAND : hi // BAND]), results[j, lo][:])
+        def scatter(j):
+            nc.vector.tensor_copy(windows[j][:].indirect(offsets[:]), results[j])
 
         def store(j):
             queue = nc.scalar if j % 2 else nc.sync
@@ -229,29 +241,28 @@ def tile_attend_gat_tnh_c_kernel(tc, qT, cT, doT, rw, qm, dom, offs, out):
             slope(t)
 
         product(psum.tile([P, half], F32, name="second2")[:], qT_mx, E4M3, 0, c_mx, E4M3, True, True, 0, half)
-        ds_woven = sbuf("ds_woven", [P, N * PACK], BF16)
+        ds_woven = [sbuf(tag, [P, half * PACK], BF16) for tag in ("ds_woven", "dom_raw0")]
         weave_block("qm", 0, nc.scalar.copy, "qm_woven0")
-        weave_slots(nc.scalar.copy, pw_woven, pw, PW_SPLIT, N)
         weave_block("dom", 0, nc.scalar.copy, "dom_woven0")
-        weave_slots(nc.scalar.copy, ds_woven, ds, DS_SPLIT, half)
-        weave_slots(nc.scalar.copy, ds_woven, ds, half, N)
+        weave_slots(nc.scalar.copy, pw_woven, pw, PW_SPLIT, N)
+        weave(nc.scalar.copy, ds_woven[1][:], ds[:, :, half:])
         quantize_block("qm", 0)
         product(psum.tile([P, N], F32, name="second1")[:], codes["qm", 0], E4M3, 0, c_mx, E4M3, True, True)
-        weave_slots(nc.vector.tensor_copy, ds_woven, ds, 0, DS_SPLIT)
+        weave(nc.vector.tensor_copy, ds_woven[0][:], ds[:, :, :half])
         first = [psum.tile([P, half], F32, name=name) for name in ("first0", "second0")]
         for bank, (lo, hi) in zip(first, halves):
             quantize(pw_mx, pw_woven, E4M3, lo, hi)
             if lo == 0:
                 quantize_block("dom", 0)
             product(bank[:], codes["dom", 0], E5M2, 0, pw_mx, E4M3, True, False, lo, hi)
-            quantize(ds_mx, ds_woven, E5M2, lo, hi)
+            nc.vector.quantize_mx(out=ds_mx[0][:, lo:hi].bitcast(E5M2), scales=ds_mx[1][:, lo:hi], in_=ds_woven[lo // half][:])
             product(bank[:], codes["qm", 0], E4M3, 0, ds_mx, E5M2, False, True, lo, hi)
 
-        flip_on_scalar(1, sbuf("pw_woven", [P, PACK, P], BF16)[:])
+        flip_on_scalar(1, sbuf("dom_woven0", [P, PACK, P], BF16)[:])
         weave_block("dom", 1, nc.vector.tensor_copy, "ds")
         weave_block("qm", 1, nc.vector.tensor_copy, "qm_woven1")
         low = sbuf("low", [P, half], F32)
-        high = sbuf("high", [P, half], F32)
+        high = sbuf("dom_woven0", [P, half], F32)
         nc.scalar.copy(out=low[:], in_=first[0][:])
         nc.scalar.activation(windows[0][:].indirect(offsets[:, : half // BAND]), low[:], ACT.Copy)
         nc.vector.tensor_copy(out=high[:], in_=first[1][:])
@@ -260,26 +271,27 @@ def tile_attend_gat_tnh_c_kernel(tc, qT, cT, doT, rw, qm, dom, offs, out):
         products(1, "dom", "qm")
         nc.vector.tensor_copy(windows[0][:].indirect(offsets[:, half // BAND :]), high[:])
         store(0)
-        flip_on_scalar(2, sbuf("low", [P, PACK, P], BF16)[:])
-        woven["dom", 2] = sbuf("qm_woven1", [P, P * PACK], BF16)[:]
+        flip_on_scalar(2, sbuf("ds", [P, PACK, P], BF16)[:])
+        shared = sbuf("qm_woven1", [P, N + P * PACK // 2], F32)
+        woven["dom", 2] = shared[:, N:].bitcast(BF16)
         nc.gpsimd.tensor_scalar(woven["dom", 2].rearrange("p (n t) -> p n t", t=PACK),
                                 rows["dom", 2].rearrange("p t n -> p n t"), 1.0, 0.0, ALU.mult, ALU.add)
-        empty(1, 0, N, "result1")
-        weave_block("qm", 2, nc.vector.tensor_copy, "high")
+        empty(1, shared[:, :N])
+        weave_block("qm", 2, nc.vector.tensor_copy, "dom_woven0")
         quantize_block("dom", 2)
-        scatter(1, 0, N)
+        scatter(1)
         store(1)
         quantize_block("qm", 2)
         products(2, "dom", "qm")
-        pair = sbuf("low", [P, 2, P * PACK], BF16)
+        pair = sbuf("ds", [P, 2, P * PACK], BF16)
         flip_on_scalar(3, pair[:, 0, :].rearrange("p (t c) -> p t c", t=PACK))
         woven["dom", 3] = pair[:, 1, :]
         weave(nc.scalar.copy, woven["dom", 3], rows["dom", 3])
-        weave_block("qm", 3, nc.vector.tensor_copy, "result1")
+        weave_block("qm", 3, nc.vector.tensor_copy, "qm_woven1")
         quantize_block("dom", 3)
         quantize_block("qm", 3)
         products(3, "dom", "qm")
-        for j, tag in ((2, "dom_raw"), (3, "result3")):
-            empty(j, 0, N, tag)
-            scatter(j, 0, N)
+        for j, tag in ((2, "dom_raw%d" % P), (3, "result3")):
+            empty(j, sbuf(tag, [P, N], F32)[:])
+            scatter(j)
             store(j)

@@ -87,7 +87,7 @@ def tile_attend_gat_tnh_c_kernel(tc, qT, cT, doT, rw, qm, dom, offs, out):
             return tile
 
         q_raw = load("qT_raw", qT, 0, PACK)
-        do_raw = [load("doT_raw%d" % h, doT, 2 * h, 2 * h + 2) for h in range(2)]
+        do_raw = load("doT_raw", doT, 0, PACK)
         raw = {}
         for lo, hi in ((0, P), (P, D)):
             for name, src in (("qm", qm), ("dom", dom)):
@@ -141,10 +141,9 @@ def tile_attend_gat_tnh_c_kernel(tc, qT, cT, doT, rw, qm, dom, offs, out):
             scores.append(bank)
 
         do_dealt = sbuf("q_dealt", [P, R * PACK], BF16)
-        for h in range(2):
-            deal(nc.vector.tensor_copy, do_dealt, do_raw[h][:], (2 * h, 2 * h + 2), (0, PACK))
+        deal(nc.vector.tensor_copy, do_dealt, do_raw[:], (0, PACK), (0, PACK))
         ds = sbuf("ds", [P, PACK, N], BF16)
-        pw = sbuf("doT_raw1", [P, PACK, N], BF16)
+        pw = sbuf("doT_raw", [P, PACK, N], BF16)
         pw_woven = sbuf("pw_woven", [P, N * PACK], BF16)
         p = [sbuf("p%d" % t, [P, N], F32) for t in range(PACK)]
         sq = [sbuf("sq%d" % t, [P, N], F32) for t in range(PACK)]

@@ -239,14 +239,12 @@ def tile_attend_gat_tnh_c_kernel(tc, qT, cT, doT, rw, qm, dom, offs, out):
         for t in range(1, PACK):
             slope(t)
 
-        product(psum.tile([P, half], F32, name="second2")[:], qT_mx, E4M3, 0, c_mx, E4M3, True, True, 0, half)
         ds_woven = [sbuf(tag, [P, half * PACK], BF16) for tag in ("ds_woven", "dom_raw0")]
         weave_block("qm", 0, nc.scalar.copy, "qm_woven0")
         weave_block("dom", 0, nc.scalar.copy, "dom_woven0")
         weave_slots(nc.scalar.copy, pw_woven, pw, PW_SPLIT, N)
         weave(nc.scalar.copy, ds_woven[1][:], ds[:, :, half:])
         quantize_block("qm", 0)
-        product(psum.tile([P, N], F32, name="second1")[:], codes["qm", 0], E4M3, 0, c_mx, E4M3, True, True)
         weave(nc.vector.tensor_copy, ds_woven[0][:], ds[:, :, :half])
         first = [psum.tile([P, half], F32, name=name) for name in ("first0", "second0")]
         for bank, (lo, hi) in zip(first, halves):

from contextlib import ExitStack

import concourse.mybir as mybir
from concourse.masks import make_identity

N, T, D, R = 512, 2048, 512, 512
FLOPS = 4 * 2 * D * R * N

F32 = mybir.dt.float32
BF16 = mybir.dt.bfloat16
U32 = mybir.dt.uint32
I32 = mybir.dt.int32
U16 = mybir.dt.uint16
U8 = mybir.dt.uint8
E4M3 = mybir.dt.float8_e4m3fn_x4
E5M2 = mybir.dt.float8_e5m2_x4
ACT = mybir.ActivationFunctionType
ALU = mybir.AluOpType

P = 128
PACK = 4
BAND = 16
RUN = 4
PW_SPLIT = 384
FLIP_SPLIT = 2
EARLY_SPLIT = 80
LATE_SPLIT = 64


def tile_attend_gat_tnh_c_kernel(tc, qT, cT, doT, rw, qm, dom, offs, out):
    nc = tc.nc
    with ExitStack() as ctx:
        keep = ctx.enter_context(tc.tile_pool(name="keep", bufs=1))
        psum = ctx.enter_context(tc.psum_pool(name="psum", bufs=1))

        def sbuf(name, shape, dtype):
            return keep.tile(shape, dtype, name=name, align_bytes=64)

        def operand(name, width):
            return sbuf(name + "_codes", [P, width], U32), sbuf(name + "_scales", [P, width], U8)

        def quantize(dst, src, fmt, lo, hi):
            codes, scales = dst
            nc.vector.quantize_mx(out=codes[:, lo:hi].bitcast(fmt), scales=scales[:, lo:hi],
                                  in_=src[:, PACK * lo : PACK * hi])

        def product(bank, stationary, stationary_fmt, lo, moving, moving_fmt, start, stop, first=0, last=N):
            nc.tensor.matmul_mx(out=bank, lhsT=stationary[0][:, lo : lo + P].bitcast(stationary_fmt),
                                lhsT_scale=stationary[1][:, lo : lo + P],
                                rhs=moving[0][:, first:last].bitcast(moving_fmt), rhs_scale=moving[1][:, first:last],
                                start=start, stop=stop)

        def weave(copy, dst, src):
            copy(out=dst.rearrange("p (c i t) -> p c t i", i=RUN, t=PACK),
                 in_=src.rearrange("p t (c i) -> p c t i", i=RUN))

        def deal(copy, dst, src, rows, places, cols=(0, P)):
            copy(out=dst[:].rearrange("p (t s j) -> p s j t", t=PACK, j=PACK)[:, cols[0] : cols[1], rows[0] : rows[1], places[0] : places[1]],
                 in_=src.rearrange("p j (s t) -> p s j t", t=PACK)[:, cols[0] : cols[1], :, places[0] : places[1]])

        halves = [(0, N // 2), (N // 2, N)]
        half = N // 2

        offsets = sbuf("offsets", [P, N // BAND], U16)
        c_rows = cT.rearrange("(p t) n -> p t n", t=PACK)
        first_two = sbuf("planes01", [P, 2, T], F32)
        nc.sync.dma_start(out=first_two[:], in_=c_rows[:, :2, :])
        gate_row = sbuf("gate_row", [P, R], F32)
        nc.gpsimd.memset(gate_row[:], 0.0)
        nc.sync.dma_start(out=gate_row[:1, :], in_=rw[0].rearrange("r o -> o r"))
        nc.sync.dma_start(offsets[:], offs)
        planes = [first_two[:, 0, :], first_two[:, 1, :]]
        for t in range(2, PACK):
            planes.append(sbuf("plane%d" % t, [P, T], F32)[:])
            nc.sync.dma_start(out=planes[t], in_=c_rows[:, t, :])
        ident = sbuf("ident", [P, P], F32)
        make_identity(nc, ident[:])
        turned = psum.tile([P, PACK, P], F32, name="first0")
        for t in range(PACK):
            nc.tensor.transpose(turned[:, t, :], gate_row[:, t::PACK], ident[:])
        gate = sbuf("gate", [P, PACK], F32)
        nc.scalar.copy(out=gate[:], in_=turned[:, :, 0])

        def load(name, src, lo, hi):
            tile = sbuf(name, [P, hi - lo, src.shape[2]], F32)
            nc.sync.dma_start(out=tile[:], in_=src[0].rearrange("(p j) w -> p j w", j=PACK)[:, lo:hi, :])
            return tile

        q_raw = load("qT_raw", qT, 0, PACK)
        do_raw = load("doT_raw", doT, 0, PACK)
        raw = {}
        for lo, hi in ((0, P), (P, D)):
            for name, src in (("qm", qm), ("dom", dom)):
                tile = sbuf("%s_raw%d" % (name, lo), [P, PACK, hi - lo], F32)
                nc.sync.dma_start(out=tile[:], in_=src[0].rearrange("(p j) w -> p j w", j=PACK)[:, :, lo:hi])
                for j in range(lo // P, hi // P):
                    raw[name, j] = tile[:, :, j * P - lo : (j + 1) * P - lo]

        windows = [sbuf("window%d" % j, [P, T], F32) for j in range(D // P)]
        for j in range(D // P - 1):
            nc.vector.memset(windows[j][:], 0.0)
        nc.gpsimd.memset(windows[D // P - 1][:], 0.0)
        size = sbuf("size", [P, PACK], F32)
        nc.scalar.activation(out=size[:], in_=gate[:], func=ACT.Abs)
        exponent = sbuf("exponent", [P, PACK], F32)
        nc.gpsimd.memset(exponent[:], 0.5)
        root = sbuf("root", [P, PACK], F32)
        nc.gpsimd.tensor_tensor(root[:], size[:], exponent[:], ALU.pow)
        level = sbuf("level", [P, PACK], F32)
        nc.gpsimd.tensor_tensor(level[:], root[:], root[:], ALU.mult)
        below = sbuf("below", [P, PACK], F32)
        nc.gpsimd.tensor_scalar(below[:], gate[:], 0.0, 2.0, ALU.is_lt, ALU.mult)
        flip = sbuf("flip", [P, PACK], F32)
        nc.gpsimd.tensor_scalar(flip[:], below[:], 1.0, -1.0, ALU.mult, ALU.add)

        c_pairs = [sbuf("c_pairs%d" % h, [P, 2, N // 2, 2], BF16) for h in range(2)]
        for t in range(PACK):
            for h, (lo, hi) in enumerate(halves):
                nc.vector.tensor_copy(c_pairs[h][:, t // 2, :, t % 2], planes[t].indirect(offsets[:, lo // BAND : hi // BAND]))
        c_woven = [sbuf("c_woven%d" % h, [P, N // 2 * PACK], BF16) for h in range(2)]
        for h in range(2):
            nc.vector.tensor_copy(out=c_woven[h][:].bitcast(I32).rearrange("p (c i u) -> p c u i", i=RUN, u=2),
                                  in_=c_pairs[h][:].rearrange("p u n e -> p u (n e)").bitcast(I32).rearrange("p u (c i) -> p c u i", i=RUN))
        c_mx = operand("c", N)
        for h, (lo, hi) in enumerate(halves):
            nc.vector.quantize_mx(out=c_mx[0][:, lo:hi].bitcast(E4M3), scales=c_mx[1][:, lo:hi], in_=c_woven[h][:])

        q_dealt = sbuf("q_dealt", [P, R * PACK], BF16)
        deal(nc.vector.tensor_copy, q_dealt, q_raw[:], (0, PACK), (0, 2), (0, EARLY_SPLIT))
        deal(nc.scalar.copy, q_dealt, q_raw[:], (0, PACK), (0, 2), (EARLY_SPLIT, P))
        deal(nc.vector.tensor_copy, q_dealt, q_raw[:], (0, PACK), (2, 4), (0, LATE_SPLIT // 2))
        deal(nc.scalar.copy, q_dealt, q_raw[:], (0, PACK), (2, 4), (LATE_SPLIT, P))
        qT_mx = operand("qT", R)
        scores = []
        for t in range(PACK):
            if t == 1:
                deal(nc.vector.tensor_copy, q_dealt, q_raw[:], (0, PACK), (2, 4), (LATE_SPLIT // 2, LATE_SPLIT))
            quantize(qT_mx, q_dealt, E4M3, t * P, (t + 1) * P)
            bank = psum.tile([P, N], F32, name="first%d" % t)
            product(bank[:], qT_mx, E4M3, t * P, c_mx, E4M3, True, True)
            scores.append(bank)

        do_dealt = sbuf("q_dealt", [P, R * PACK], BF16)
        deal(nc.vector.tensor_copy, do_dealt, do_raw[:], (0, PACK), (0, PACK))
        ds = sbuf("ds", [P, PACK, N], BF16)
        pw = sbuf("doT_raw", [P, PACK, N], BF16)
        pw_woven = sbuf("pw_woven", [P, N * PACK], BF16)
        p = [sbuf("p%d" % t, [P, N], F32) for t in range(PACK)]
        sq = [sbuf("sq%d" % t, [P, N], F32) for t in range(PACK)]
        for t in range(PACK):
            nc.scalar.activation(out=p[t][:], in_=scores[t][:], func=ACT.Tanh)

        def square(t):
            nc.scalar.activation(out=sq[t][:], in_=p[t][:], func=ACT.Square, scale=root[:, t : t + 1])

        for t in range(PACK - 1):
            square(t)

        def weave_slots(copy, dst, src, lo, hi):
            weave(copy, dst[:, PACK * lo : PACK * hi], src[:, :, lo:hi])

        def gated(t):
            nc.vector.tensor_scalar(pw[:, t, :], p[t][:], gate[:, t : t + 1], None, ALU.mult)

        def slope(t):
            nc.vector.scalar_tensor_tensor(ds[:, t, :], sq[t][:], level[:, t : t + 1], dp[t][:], ALU.subtract, ALU.mult)

        pw_mx = operand("pw", N)
        ds_mx = operand("ds", N)
        rows = {}
        woven = {}
        codes = {}

        def flip_on_vector(j, flipped, places):
            for t in places:
                nc.vector.tensor_scalar(flipped[:, t, :], raw["qm", j][:, t, :], flip[:, t : t + 1], None, ALU.mult)

        for j in range(D // P):
            rows["dom", j] = raw["dom", j]

        def weave_block(name, j, copy, tag):
            woven[name, j] = sbuf(tag, [P, P * PACK], BF16)[:]
            weave(copy, woven[name, j], rows[name, j])

        def flip_on_scalar(j, flipped, places=range(PACK)):
            for t in places:
                nc.scalar.activation(out=flipped[:, t, :], in_=raw["qm", j][:, t, :], func=ACT.Copy,
                                     scale=flip[:, t : t + 1])
            rows["qm", j] = flipped

        def quantize_block(name, j):
            codes[name, j] = operand("%s%d" % (name, j), P)
            quantize(codes[name, j], woven[name, j], E4M3 if name == "qm" else E5M2, 0, P)

        banks = {}
        results = {}

        def products(j, first, second):
            moving = {"dom": (E5M2, pw_mx, E4M3), "qm": (E4M3, ds_mx, E5M2)}
            banks[j] = psum.tile([P, N], F32, name="first%d" % j)
            for name in (first, second):
                product(banks[j][:], codes[name, j], moving[name][0], 0, moving[name][1], moving[name][2],
                        name == first, name == second)

        def empty(j, result):
            results[j] = result
            nc.scalar.copy(out=result, in_=banks[j][:])

        def scatter(j):
            nc.vector.tensor_copy(windows[j][:].indirect(offsets[:]), results[j])

        def store(j):
            queue = nc.scalar if j % 2 else nc.sync
            queue.dma_start(out=out[j * P : (j + 1) * P, :], in_=windows[j][:])

        doT_mx = operand("doT", R)
        dp = []

        def gradient(t):
            dp.append(psum.tile([P, N], F32, name="second%d" % (t % (PACK - 1))))
            product(dp[t][:], doT_mx, E5M2, t * P, c_mx, E4M3, True, True)

        gated(0)
        for t in range(PACK):
            quantize(doT_mx, do_dealt, E5M2, t * P, (t + 1) * P)
            if t < PACK - 1:
                gradient(t)
        for t in range(1, PACK - 1):
            gated(t)
        flipped0 = sbuf("flipped0", [P, PACK, P], BF16)
        flip_on_vector(0, flipped0[:], range(FLIP_SPLIT))
        flip_on_scalar(0, flipped0[:], range(FLIP_SPLIT, PACK))
        square(PACK - 1)
        gated(PACK - 1)
        nc.gpsimd.tensor_scalar(pw_woven[:, : PACK * PW_SPLIT].rearrange("p (n t) -> p n t", t=PACK),
                                pw[:, :, :PW_SPLIT].rearrange("p t n -> p n t"), 1.0, 0.0, ALU.mult, ALU.add)
        slope(0)
        gradient(PACK - 1)
        for t in range(1, PACK):
            slope(t)

        ds_woven = [sbuf(tag, [P, half * PACK], BF16) for tag in ("ds_woven", "dom_raw0")]
        weave_block("qm", 0, nc.scalar.copy, "qm_woven0")
        weave_block("dom", 0, nc.scalar.copy, "dom_woven0")
        weave_slots(nc.scalar.copy, pw_woven, pw, PW_SPLIT, N)
        weave(nc.scalar.copy, ds_woven[1][:], ds[:, :, half:])
        quantize_block("qm", 0)
        weave(nc.vector.tensor_copy, ds_woven[0][:], ds[:, :, :half])
        first = [psum.tile([P, half], F32, name=name) for name in ("first0", "second0")]
        for bank, (lo, hi) in zip(first, halves):
            quantize(pw_mx, pw_woven, E4M3, lo, hi)
            if lo == 0:
                quantize_block("dom", 0)
            product(bank[:], codes["dom", 0], E5M2, 0, pw_mx, E4M3, True, False, lo, hi)
            nc.vector.quantize_mx(out=ds_mx[0][:, lo:hi].bitcast(E5M2), scales=ds_mx[1][:, lo:hi], in_=ds_woven[lo // half][:])
            product(bank[:], codes["qm", 0], E4M3, 0, ds_mx, E5M2, False, True, lo, hi)

        flip_on_scalar(1, sbuf("dom_woven0", [P, PACK, P], BF16)[:])
        weave_block("dom", 1, nc.vector.tensor_copy, "ds")
        weave_block("qm", 1, nc.vector.tensor_copy, "qm_woven1")
        low = sbuf("low", [P, half], F32)
        high = sbuf("dom_woven0", [P, half], F32)
        nc.scalar.copy(out=low[:], in_=first[0][:])
        nc.scalar.activation(windows[0][:].indirect(offsets[:, : half // BAND]), low[:], ACT.Copy)
        nc.vector.tensor_copy(out=high[:], in_=first[1][:])
        quantize_block("dom", 1)
        quantize_block("qm", 1)
        products(1, "dom", "qm")
        nc.vector.tensor_copy(windows[0][:].indirect(offsets[:, half // BAND :]), high[:])
        store(0)
        flip_on_scalar(2, sbuf("ds", [P, PACK, P], BF16)[:])
        shared = sbuf("qm_woven1", [P, N + P * PACK // 2], F32)
        woven["dom", 2] = shared[:, N:].bitcast(BF16)
        nc.gpsimd.tensor_scalar(woven["dom", 2].rearrange("p (n t) -> p n t", t=PACK),
                                rows["dom", 2].rearrange("p t n -> p n t"), 1.0, 0.0, ALU.mult, ALU.add)
        empty(1, shared[:, :N])
        weave_block("qm", 2, nc.vector.tensor_copy, "dom_woven0")
        quantize_block("dom", 2)
        scatter(1)
        store(1)
        quantize_block("qm", 2)
        products(2, "dom", "qm")
        pair = sbuf("ds", [P, 2, P * PACK], BF16)
        flip_on_scalar(3, pair[:, 0, :].rearrange("p (t c) -> p t c", t=PACK))
        woven["dom", 3] = pair[:, 1, :]
        weave(nc.scalar.copy, woven["dom", 3], rows["dom", 3])
        weave_block("qm", 3, nc.vector.tensor_copy, "qm_woven1")
        quantize_block("dom", 3)
        quantize_block("qm", 3)
        products(3, "dom", "qm")
        for j, tag in ((2, "dom_raw%d" % P), (3, "result3")):
            empty(j, sbuf(tag, [P, N], F32)[:])
            scatter(j)
            store(j)
